import numpy as np, ml_dtypes
CORES = [5,29,101,125,133,157,229,253]
N = 8
import mx_ref
BF = ml_dtypes.bfloat16
def gcols(t, e):
    v = np.concatenate([t.reshape(8, 16, -1, 4), np.zeros((8, 16, 1, 4), BF)], axis=2)
    return np.ascontiguousarray(np.stack([v[g][:, e[g]] for g in range(8)])).reshape(128, -1)
def tile(rs):
    return np.stack(rs, axis=2).reshape(128, -1).astype(BF)
def pick(q, e):
    c = np.concatenate([q[0].reshape(128, -1, 4), np.zeros((128, 1, 4), np.uint8)], axis=1); s = np.concatenate([q[1], np.ones((16, 1), np.uint8)], axis=1)
    return (np.ascontiguousarray(c[:, e].reshape(128, -1)), np.ascontiguousarray(s[:, e]))
def join(*qs):
    return (np.concatenate([q[0] for q in qs], axis=1), np.concatenate([q[1] for q in qs], axis=1))
def put(q, e, v):
    c, s = q[0].reshape(128, -1, 4).copy(), q[1].copy(); c[:, e] = v[0].reshape(128, -1, 4); s[:, e] = v[1]
    return (c.reshape(128, -1), s)
def pk(c, s):
    return (np.ascontiguousarray(c), mx_ref.live(s))
def emit(q):
    return q[0], q[1]
def packed(v, rng):
    q = [mx_ref.quantize(np.ascontiguousarray(v[r])) for r in range(N)]
    return np.stack([a for a, b in q]), np.stack([mx_ref.plane(b, rng) for a, b in q])
def values_of_codes():
    e, c = np.zeros((128, 128, 4), np.float32), np.zeros((128, 2, 4), np.uint8)
    e[np.arange(128), np.arange(128), 0] = 1
    c[:127, :, 0] = np.arange(256).reshape(2, 128).T[:127]
    return mx_ref.matmul(mx_ref.quantize(e.reshape(128, 512).astype(BF)), (c.reshape(128, 8), np.full((16, 2), 127, np.uint8))).T.reshape(-1).astype(np.float64)
CODE_VALUE, SCALE_VALUE = values_of_codes(), 2.0 ** (np.arange(256) - 127.0)
def decode(q):
    return (CODE_VALUE[q[0]].reshape(16, 8, -1, 4) * SCALE_VALUE[q[1]][:, None, :, None] + 0.0).reshape(128, -1).astype(np.float32)
def f(rng, *shape):
    return mx_ref.flush((rng.standard_normal(shape, dtype=np.float32) * np.exp2(rng.integers(-2, 3, shape[:-1] + (1,)))).astype(BF))
def wide(rng, *shape, cols=0):
    v = rng.standard_normal(shape, dtype=np.float32) * np.exp2(rng.integers(-12, 13, shape)).astype(np.float32)
    if cols: v *= np.repeat(np.exp2(rng.integers(-cols, cols + 1, shape[:-2] + (1, shape[-1] // 4))) * (rng.random(shape[:-2] + (1, shape[-1] // 4)) > 0.0625), 4, axis=-1).astype(np.float32)
    return mx_ref.flush(v.astype(BF))
C, L, S, M, R = 320, 96, 6, 5, 3
STEP = [1, 2, 4]
def park(p):
    home = np.zeros((8, C), np.int64)
    for b in range(S): home += (p[b::16] > 0) * (M << b)
    o = np.lexsort((-(p[8::16] + np.float32(0.0)), home))
    h = np.take_along_axis(home, o, 1)
    i = np.arange(C)
    place = i + np.maximum.accumulate(h - i, axis=1)
    over = place >= C
    for g in range(8): place[g, over[g]] = np.flatnonzero(~np.isin(i, place[g]))
    gap = place + C * over - h
    e = np.lexsort((place, -gap))[:, :L]
    m = np.zeros((8, C), np.int64)
    np.put_along_axis(m, place, o, 1)
    return m, np.take_along_axis(o, e, 1), np.take_along_axis(place, e, 1)
def numbers_of(rng):
    return {"x": np.array(f(rng, N, 128, 4 * C)), "u": np.array(f(rng, N, 128, 512)), "v": np.array(f(rng, N, 128, 512))}
def weights(rng, still=[], positive=False):
    w = np.array(f(rng, N, 128, 2048)).reshape(N, 8, 16, 4, 8, 16, 4)
    if positive: w = np.abs(w.astype(np.float32)).astype(BF)
    for i in still:
        w[:, :, i] = 0
        w[:, :, :, :, :, i] = 0
    c, p = packed(w.reshape(N, 128, 2048), rng)
    return {"wc": c, "ws": p}
def signs(rng):
    return np.stack([rng.permutation(8) % 2 * 2.0 - 1.0 for r in range(N)])
def setup_inputs(rng):
    return {**numbers_of(rng), **weights(rng)}
def setup_inputs_ties(rng):
    d = numbers_of(rng)
    e = rng.permutation(N)
    x = d["x"].reshape(N, 8, 16, C, 4)
    for r in range(N):
        k = np.zeros(C, int) if r == e[0] else rng.permutation(C) % 3
        a = x[r][:, :8, :3].copy()
        a[:, :, 2] = 0
        x[r][:, :8] = a[:, :, k]
    x[e[1]] = 0
    u = d["u"].reshape(N, 8, 16, 8, 16, 4)
    k = u.copy()
    u[:, :, :, :, :9] = 0
    for g in range(8): u[:, g, :8, g, :9] = k[:, g, :8, g, :9]
    return {"x": x.reshape(N, 128, 4 * C), "u": u.reshape(N, 128, 512), "v": d["v"], **weights(rng, range(8))}
def setup_inputs_near(rng):
    d = numbers_of(rng)
    x = np.zeros((N, 8, 16, C, 4), np.float32)
    u = d["u"].reshape(N, 8, 16, 8, 16, 4)
    u[:, :, :, :, :9] = 0
    o, c = rng.permutation(N) % 4, signs(rng)
    j = np.arange(C)
    upper = j // (C // 2)
    for r in range(N):
        i = (j + rng.integers(0, C, (8, 1))) % C
        if o[r] == 3: i = i % (C // 2) * 2 + upper
        z = rng.integers(0, 1 << S, (8, 8))[np.arange(8)[:, None], i // (C // 8)]
        k = 1.0 if o[r] == 0 else 2.0 ** -30
        size = 1.0 if o[r] < 2 else 2.0 ** -4
        for b in range(S): x[r, :, b, :, 0] = np.where((z >> b) & 1, k, -k * rng.integers(0, 2, (8, C)))
        if o[r] < 2: x[r, :, 7, :, 0] = k * np.where(c[r] > 0, 1.0, -1.5)[:, None]
        if o[r] == 3: x[r, :, 7, :, 0] = (8 + upper) * 2.0 ** -33
        a = (((i // 2)[:, :, None] >> np.arange(8)) & 1) * np.exp2(np.arange(8) - 23.0) * size
        x[r, :, 8] = a[:, :, :4]
        x[r, :, 9] = a[:, :, 4:]
        if o[r] < 2:
            for g in rng.permutation(8)[:4]: x[r, g, 11, rng.integers(C), 0] = 2.0 ** 30
        x[r, :, 12:] = rng.integers(4, 8, (8, 4, C, 4)) * 2.0 ** -20 * size
        for g in range(8):
            for b in range(S): u[r, g, b, g, b, 0] = k
            u[r, g, 7, g, 8, 0] = 1.0 if o[r] < 2 else k
            u[r, g, 8:10, g, 8] = k
            u[r, g, 11, g, 8, 0] = k
    return {"x": x.reshape(N, 128, 4 * C).astype(BF), "u": u.reshape(N, 128, 512), "v": d["v"], **weights(rng, range(12), True)}
def setup_inputs_huge(rng):
    d = numbers_of(rng)
    x = 2.0 ** 30 * (0.8 + 0.2 * rng.random((N, 128, C, 4)))
    c = np.ones((N, C))
    half = int(rng.integers(2))
    for r in range(N):
        if 2 * r // N == half: c[r] = rng.permutation(C) % 2 * 2.0 - 1.0
    x *= c[:, None, :, None]
    a = 2.0 ** 30 * (1 - 0.1 * rng.random((N, 128, 8, 4))) * signs(rng)[:, None, :, None]
    u = d["u"].reshape(N, 8, 16, 8, 16, 4)
    u[:, :, :, :, :9] = 0
    u[:, :, :, :, 8] = a.astype(np.float32).astype(BF).reshape(N, 8, 16, 8, 4)
    e = (2.0 ** 30 * rng.choice([-1.0, 1.0], (N, 8, S))).astype(np.float32).astype(BF)
    for g in range(8): u[:, g, :, g, :S] = e[:, g][:, None, :, None]
    w = np.zeros((N, 128, 4, 128, 4), np.float32)
    i = np.arange(128)
    for b in range(4): w[:, i, b, i, b] = -1
    wc, ws = packed(w.reshape(N, 128, 2048).astype(BF), rng)
    return {"x": x.astype(np.float32).reshape(N, 128, 4 * C).astype(BF), "u": u.reshape(N, 128, 512), "v": d["v"], "wc": wc, "ws": ws}
def setup_inputs_homes(rng):
    d = numbers_of(rng)
    x = d["x"].astype(np.float32).reshape(N, 8, 16, C, 4)
    u = d["u"].reshape(N, 8, 16, 8, 16, 4)
    x[:, :, :8] = 0
    u[:, :, :, :, :S] = 0
    last = (1 << S) - 1
    small = rng.permutation(N) < N // 2
    for r in range(N):
        k = 2.0 ** -30 if small[r] else 1.0
        one = np.arange(C) // M
        one[rng.integers(C - M)] = last
        case = [np.zeros(C, int), np.full(C, last), np.arange(C) // M, one, np.arange(C) // (C // 2) * last, np.full(C, rng.integers(last + 1))]
        for n in (L, L + 1): case.append(np.concatenate([np.arange(C - M - n) // M, np.full(M + n, last)]))
        o = rng.permutation(8)
        x[r, :, 7, :, 0] = -k
        for g in range(8):
            z = rng.permutation(case[o[g]])
            for b in range(S):
                x[r, g, b, :, 0] = k * np.where((z >> b) & 1, 1.125, rng.integers(0, 2, C))
                u[r, g, b, g, b, 0] = k
                u[r, g, 7, g, b, 0] = k
    return {"x": x.reshape(N, 128, 4 * C).astype(BF), "u": u.reshape(N, 128, 512), "v": d["v"], **weights(rng, range(8))}
def setup_inputs_spread(rng):
    d = setup_inputs(rng)
    d["x"] = wide(rng, N, 128, 4 * C, cols=6)
    return d
def check_inputs(d):
    b = []
    for k in ("x", "u", "v"):
        a = np.abs(d[k].astype(np.float32))
        if not (np.isfinite(a).all() and ((a == 0) | (a >= 2.0 ** -30) & (a <= 2.0 ** 30)).all()): b.append("a value of " + k)
    if ((d["wc"] & 0x7F) == 0x7F).any(): b.append("a code of wc that is no number")
    z = np.zeros((128, 4, 4), np.float32)
    z[:, 1] = 2.0 ** -30
    z[:, 2] = 2.0 ** 30
    c, s = emit(mx_ref.quantize(z.reshape(128, 16).astype(BF)))
    for r in range(N):
        p = mx_ref.live(d["ws"][r])
        if not ((p == s[0, 0]) | (p >= s[0, 1]) & (p <= s[0, 2])).all(): b.append("a scale of ws")
    return b
def reference(x, u, v, wc, ws):
    qu = [mx_ref.quantize(u[r]) for r in range(N)]
    lay = [pk(wc[r], ws[r]) for r in range(N)]
    now = [x[r] for r in range(N)]
    for t in range(R):
        sent, m = [], []
        for r in range(N):
            e, b, a = park(mx_ref.matmul(qu[r], mx_ref.quantize(now[r])))
            sent.append(mx_ref.quantize(gcols(now[r], b)))
            np.put_along_axis(e, a, np.tile(C + np.arange(L), (8, 1)), 1)
            m.append(e)
        made = []
        for r in range(N):
            came = decode(sent[(r - STEP[t]) % N]).astype(BF)
            c = gcols(np.concatenate([now[r], came], axis=1), m[r])
            q = mx_ref.quantize(c)
            made.append(tile([mx_ref.matmul(pick(lay[r], np.arange(128 * b, 128 * b + 128)), q) * np.float32(0.015625) + c[:, b::4].astype(np.float32) for b in range(4)]))
        now = made
    y, ot = np.zeros((N, 128, C), np.float32), np.zeros((N, 8, C), np.float32)
    oc, osc = np.zeros((N, 128, 4 * C), np.uint8), np.zeros((N, 16, C), np.uint8)
    for r in range(N):
        q = mx_ref.quantize(now[r])
        y[r] = mx_ref.matmul(mx_ref.quantize(v[r]), q)
        ot[r] = m[r]
        oc[r], osc[r] = emit(q)
    return {"y": y, "ot": ot, "oc": oc, "osc": osc}

@@ -1,0 +1,495 @@
+from concourse.mybir import dt, AluOpType, AxisListType, ActivationFunctionType
+
+ALU = AluOpType
+ACT = ActivationFunctionType
+C, L, R = 320, 96, 3
+STEP = [1, 2, 4]
+K = 262144.0
+BIG = 32 * K
+F32, BF, I32, U16, X4, U8 = "float32", "bfloat16", "int32", "uint16", "float8_e4m3fn_x4", "uint8"
+T4, T3, T2, TU = 0, 1280, 2304, 3072
+Q4, Q3, Q2, QU = 0, 256, 448, 576
+
+SCRATCH = {}
+
+
+def _sb(name, n, d):
+    SCRATCH[name] = ("sbuf", [128, n], d)
+
+
+def _pair(name, n):
+    _sb("q" + name, n, X4)
+    _sb("s" + name, n, U8)
+
+
+for _t in range(R + 1):
+    _sb("tw%d" % _t, 4 * C + 4 * L, BF)
+    _pair("T%d" % _t, C)
+for _t in range(R):
+    _pair("L%d" % _t, C)
+    _pair("R%d" % _t, C)
+    for _n in ("ll", "rl", "sl"):
+        _sb("%s%d" % (_n, _t), 24, U16)
+for _n, _w in (("u", 128), ("S", 128), ("v", 128), ("w", 512), ("one", 128), ("E", 512), ("bits", C), ("hs", C),
+               ("V", C), ("A", 960), ("B", 960), ("C", 960)):
+    _pair(_n, _w)
+for _n, _w in (("ub", 512), ("vb", 512), ("j16", C), ("g8", 512), ("one", 512), ("ones", 512), ("E", 2048), ("j4", C),
+               ("mask", C), ("nmask", C), ("nm4", C), ("M16", C), ("M4", C), ("Mr", 240),
+               ("io2", C), ("bits", 4 * C), ("hs", 4 * C), ("tA", 4608), ("tB", 4608), ("tC", 4608),
+               ("D", 4 * C), ("V", 4 * C), ("V64", 4 * C)):
+    _sb(_n, _w, BF)
+for _n, _w in (("I", 328), ("J", 648), ("c80", 80), ("cf", 4), ("col", 24), ("pw", 24), ("kw", 48), ("crow", C), ("krow", C),
+               ("c64", 64), ("TL", C), ("cx", 400), ("CX", 240), ("sm", C), ("sx", C), ("eh", C), ("hk", C), ("acc", 72),
+               ("ext", 3 * C), ("Z", 136), ("EX", 240), ("EY", 240), ("sm2", 240), ("X", C), ("kB", C), ("kC", C), ("eC", C),
+               ("orow", C), ("mrow", C), ("brow", C), ("otr", C), ("eo", C + L), ("tmp", 4 * C), ("yb", C)):
+    _sb(_n, _w, F32)
+for _n, _w in (("ip", 16), ("q5", 16)):
+    _sb(_n, _w, I32)
+for _n, _w in (("pk", 8), ("xl", 16), ("ul", 88), ("off", 80)):
+    _sb(_n, _w, U16)
+for _b in range(8):
+    SCRATCH["ps%d" % _b] = ("psum", [128, 512], F32)
+
+SEMAPHORES = ["ev", "es", "et", "eg", "dx", "du", "dw", "dv", "dout", "sent"] + \
+    ["%s%d" % (_n, _t) for _n in ("aq", "al") for _t in range(R)]
+
+
+def _engines(m):
+    return bin(m).count("1")
+
+
+def _route(src, dst, topo):
+    if topo.may_write(src, dst):
+        return [src, dst]
+    able = [c for c in topo.cores_of(src) if c != src and topo.may_write(c, dst)]
+    near = [c for c in able if topo.die(c) == topo.die(src)]
+    return [src, (near or able)[0], dst]
+
+
+def _hop(g, T, topo, src, dst, out, in_, sem):
+    rid, pid = topo.addr(dst, src)
+    m = topo.mask(src, dst)
+    g.remote_dma(out, in_, T.sem[sem], T.sem.sent, pid, rid, m)
+    return _engines(m)
+
+
+def _relay(g, core, T, topo):
+    n = len(T.cores)
+    sent = 0
+    for t in range(R):
+        for r in range(n):
+            way = _route(T.cores[r], T.cores[(r + STEP[t]) % n], topo)
+            if len(way) == 3 and way[1] == core:
+                e = _engines(topo.mask(way[0], core))
+                g.wait_ge(T.sem["aq%d" % t], 2 * e)
+                sent += _hop(g, T, topo, core, way[2], T["qL%d" % t][:].bitcast(dt.uint8), T["qR%d" % t][:].bitcast(dt.uint8), "aq%d" % t)
+                sent += _hop(g, T, topo, core, way[2], T["sL%d" % t][:], T["sR%d" % t][:], "aq%d" % t)
+                g.wait_ge(T.sem["al%d" % t], e)
+                sent += _hop(g, T, topo, core, way[2], T["ll%d" % t][:], T["rl%d" % t][:], "al%d" % t)
+    if sent:
+        g.wait_ge(T.sem.sent, sent)
+
+
+def rank_program(g, core, T, topo):
+    rank = T.rank_of(core)
+    if rank is None:
+        _relay(g, core, T, topo)
+        return
+    n = len(T.cores)
+    Q = {"v": g.vector, "s": g.scalar, "t": g.tensor, "g": g, "y": g.sync}
+    SEM = {"v": "ev", "s": "es", "t": "et", "g": "eg"}
+    count = {}
+    clock = {e: {} for e in Q}
+    log = {}
+
+    def a(name, lo=0, hi=None, st=1):
+        if hi is None:
+            hi = SCRATCH[name][1][1]
+        ap = T[name][:, lo:hi] if st == 1 else T[name][:, lo:hi:st]
+        if name.startswith("ps"):
+            return (ap, [(name, frozenset([0]))])
+        return (ap, [(name, frozenset(range(lo, hi, st)))])
+
+    def c1(name, j):
+        return a(name, j, j + 1)
+
+    def ind(win, off):
+        return (win[0].indirect(off[0]), win[1] + off[1])
+
+    def order(e, reads, writes):
+        need = {}
+        for kind, accs in (("r", reads), ("w", writes)):
+            for x in accs:
+                for name, cols_ in x[1]:
+                    for k, c, who, sem, val, snap in log.get(name, []):
+                        both = k == "r" and kind == "r" and (who == e or not name.startswith("ps"))
+                        chain = name.startswith("ps") and who == e and k == kind
+                        if both or chain or c.isdisjoint(cols_):
+                            continue
+                        if val > need.get(sem, (0, None))[0]:
+                            need[sem] = (val, snap)
+        for sem in sorted(need, key=lambda s: -len(need[s][1])):
+            val, snap = need[sem]
+            if clock[e].get(sem, 0) < val:
+                Q[e].wait_ge(T.sem[sem], val)
+                for s, v in snap.items():
+                    clock[e][s] = max(clock[e].get(s, 0), v)
+
+    def note(e, reads, writes, sem, inc):
+        count[sem] = count.get(sem, 0) + inc
+        snap = dict(clock[e]) if e in clock else {}
+        snap[sem] = count[sem]
+        for kind, accs in (("r", reads), ("w", writes)):
+            for x in accs:
+                for name, cols_ in x[1]:
+                    old = log.get(name, [])
+                    if kind == "w":
+                        old = [o for o in old if not o[1] <= cols_]
+                    log[name] = old + [(kind, cols_, e, sem, count[sem], snap)]
+
+    def op(e, reads, writes, call):
+        reads = [x for x in reads if isinstance(x, tuple)]
+        order(e, reads, writes)
+        call().then_inc(T.sem[SEM[e]], 1)
+        note(e, reads, writes, SEM[e], 1)
+
+    def p(x):
+        return x[0] if isinstance(x, tuple) else x
+
+    def ts(out, in0, s1, op0, s2=None, op1=None):
+        if op1 is None:
+            op("v", [in0, s1], [out], lambda: g.vector.tensor_scalar(out[0], in0[0], p(s1), None, op0))
+        else:
+            op("v", [in0, s1, s2], [out], lambda: g.vector.tensor_scalar(out[0], in0[0], p(s1), p(s2), op0, op1))
+
+    def tt(out, in0, in1, o):
+        op("v", [in0, in1], [out], lambda: g.vector.tensor_tensor(out[0], in0[0], in1[0], o))
+
+    def cp(out, in_):
+        op("v", [in_], [out], lambda: g.vector.tensor_copy(out[0], in_[0]))
+
+    def scatter(win, off, in_):
+        op("v", [in_, off], [win], lambda: g.vector.tensor_copy(win[0].indirect(off[0]), in_[0]))
+
+    def scan(out, d0, d1, init, op0, op1):
+        op("v", [d0, d1], [out], lambda: g.vector.tensor_tensor_scan(out[0], d0[0], d1[0], init, op0, op1))
+
+    def fill(out, v):
+        op("v", [], [out], lambda: g.vector.memset(out[0], v))
+
+    def quant(name, lo, hi, in_):
+        q, s = a("q" + name, lo, hi), a("s" + name, lo, hi)
+        op("v", [in_], [q, s], lambda: g.vector.quantize_mx(q[0], s[0], in_[0]))
+
+    def mm(bank, st, slo, mv, lo, hi, start=True, stop=True):
+        o = a("ps%d" % bank, 0, hi - lo)
+        x = [a("q" + st, slo, slo + 128), a("s" + st, slo, slo + 128), a("q" + mv, lo, hi), a("s" + mv, lo, hi)]
+        op("t", x, [o], lambda: g.tensor.matmul_mx(o[0], x[0][0], x[1][0], x[2][0], x[3][0], start, stop))
+
+    def act(out, in_, f, bias=None, scale=1.0, acc=None):
+        kw = {"scale": p(scale)}
+        if bias is not None:
+            kw["bias"] = p(bias)
+        if acc is not None:
+            kw["accum_out"] = acc[0]
+        op("s", [in_, bias, scale], [out] + ([acc] if acc else []), lambda: g.scalar.activation(out[0], in_[0], f, **kw))
+
+    def lin(out, in_, scale, bias):
+        act(out, in_, ACT.Identity, bias, scale)
+
+    def iota(out, pattern, base=0, cm=0):
+        if SCRATCH[out[1][0][0]][2] == I32:
+            op("g", [], [out], lambda: g.iota(out[0], pattern, base, cm))
+        else:
+            op("g", [], [out], lambda: g.iota(out[0], pattern, base, cm, allow_small_or_imprecise_dtypes=True))
+
+    def dma(e, out, in_, reads, writes, sem):
+        order(e, reads, writes)
+        Q[e].dma_start(out, in_).then_inc(T.sem[sem], 16)
+        note(e, reads, writes, sem, 16)
+
+    def ps(b, w=C):
+        return a("ps%d" % b, 0, w)
+
+    def send(t, what, src):
+        way = _route(core, T.cores[(rank + STEP[t]) % n], topo)
+        relay = len(way) == 3
+        order("g", [src], [])
+        if what == "l":
+            e = _hop(g, T, topo, core, way[1], T[("rl%d" if relay else "ll%d") % t][:], src[0], "al%d" % t)
+        else:
+            out = T[what + ("R%d" if relay else "L%d") % t][:]
+            if what == "q":
+                e = _hop(g, T, topo, core, way[1], out.bitcast(dt.uint8), src[0].bitcast(dt.uint8), "aq%d" % t)
+            else:
+                e = _hop(g, T, topo, core, way[1], out, src[0], "aq%d" % t)
+        count["sent"] = count.get("sent", 0) + e
+
+    for t in range(R):
+        e = _engines(topo.mask(_route(T.cores[(rank - STEP[t]) % n], core, topo)[-2], core))
+        note("far", [], [a("qL%d" % t), a("sL%d" % t)], "aq%d" % t, 2 * e)
+        note("far", [], [a("ll%d" % t)], "al%d" % t, e)
+
+    dma("y", a("tw0", 0, 4 * C)[0], T.x[:], [], [a("tw0", 0, 4 * C)], "dx")
+    dma("s", T.ub[:], T.u[:], [], [a("ub")], "du")
+    dma("y", T.qw[:].bitcast(dt.uint8), T.wc[:], [a("tw0", 0, 8)], [], "dw")
+    dma("y", T.sw[:], T.ws[:], [], [a("qw"), a("sw")], "dw")
+    dma("y", T.vb[:], T.v[:], [], [a("vb")], "dv")
+
+    c0, cg, c2, c3 = (c1("cf", j) for j in range(4))
+    (K16, c4a, col4, colA, colB, w3, m15, c820, powc, cfix) = (c1("col", j) for j in range(10))
+    kwc, constw, thrb = a("kw", 0, 20), a("kw", 20, 40), a("kw", 40, 44)
+    cc, h5, w5, aw, pen = (a("cx", 80 * j, 80 * j + 80) for j in range(5))
+    iota(a("ip", 0, 1), [[0, 1]], 0, 1)
+    iota(a("j16"), [[0, 20], [1, 16]])
+    iota(a("ip", 8, 16), [[16, 8]], 8, 0)
+    iota(a("I"), [[1, 328]])
+    iota(a("c80"), [[16, 20], [0, 4]])
+    iota(a("q5", 0, 5), [[64 * 205, 5]])
+    iota(a("j4"), [[0, 80], [4, 4]])
+    iota(a("g8"), [[1, 8], [0, 64]])
+    iota(a("J"), [[1, 648]])
+    fill(a("bits"), 0.0)
+    ts(c1("ip", 4), c1("ip", 0), 15, ALU.bitwise_and)
+    ts(c1("ip", 5), c1("ip", 0), 4, ALU.logical_shift_right)
+    ts(c1("ip", 6), c1("ip", 0), 3, ALU.bitwise_and)
+    ts(c1("ip", 7), c1("ip", 0), 12, ALU.bitwise_and)
+    fill(a("pw", 0, 6), 2.0)
+    cp(a("cf"), a("ip", 4, 8))
+    scan(a("pw", 8, 14), a("pw", 0, 6), a("pw", 0, 6), 320.0, ALU.mult, ALU.max)
+    cp(a("pk"), a("ip", 8, 16))
+    ts(a("mask"), a("j16"), c0, ALU.is_equal)
+    ts(a("nmask"), a("j16"), c0, ALU.not_equal)
+    lin(c820, c3, 820.0, 0.0)
+    lin(K16, c0, -K, 15 * K)
+    lin(c4a, c3, K, c2)
+    lin(w3, c1("mask", 15), 166400.0, -2560.0)
+    lin(m15, c1("mask", 15), 2.0, 0.0)
+    lin(a("M16"), a("nmask"), K + BIG, -BIG)
+    lin(colA, K16, -1.0, 320.0)
+    lin(colB, K16, -0.5, 159.5)
+    lin(col4, c4a, 1.0, -12 * K)
+    tt(a("pw", 16, 22), a("pw", 8, 14), a("mask", 0, 6), ALU.mult)
+    fill(a("acc", 0, 8), 127.0)
+    fill(a("acc", 48, 56), 191.0)
+    op("v", [a("pw", 16, 22)], [powc], lambda: g.vector.tensor_reduce(powc[0], a("pw", 16, 22)[0], AxisListType.X, ALU.add, negate=True))
+    fill(c1("Z", 64), 0.0)
+    fill(a("TL", L, C), 0.0)
+    lin(a("crow"), a("I", 0, C), -1.0 / 512, 20480.0)
+    lin(kwc, a("c80", 0, 80, 4), 1.0, c0)
+    lin(cc, a("c80"), 1.0, c0)
+    lin(a("c64"), a("I", 0, 64), 5.0, 5.0)
+    lin(thrb, a("kw", 0, 4), 640.0, 320.0)
+    lin(constw, kwc, -1.0 / 512, 20160.0)
+    ts(a("q5", 8, 13), a("q5", 0, 5), c820, ALU.add)
+    ts(a("q5", 8, 13), a("q5", 8, 13), 10, ALU.logical_shift_right)
+    ts(a("xl", 0, 5), a("q5", 8, 13), c2, ALU.add)
+    ts(a("xl", 5, 10), a("q5", 8, 13), c2, ALU.add, 64.0, ALU.add)
+    ts(a("xl", 10, 15), a("q5", 8, 13), c2, ALU.add, 64.0, ALU.add)
+    ts(h5, ind(a("I", 0, 64), a("xl", 0, 5)), 5.0, ALU.mult, 5.0, ALU.add)
+    quant("u", 0, 128, a("ub"))
+    tt(w5, cc, h5, ALU.subtract)
+    pick = a("pk")
+    op("v", [a("qu"), pick], [a("qS")], lambda: g.vector.tensor_copy(T.qS[:].bitcast(dt.uint32), T.qu[:].bitcast(dt.uint32).indirect(pick[0])))
+    for j in range(3):
+        lin(a("ext", j * C + 256, (j + 1) * C), a("I", 0, 64), 0.0, K16)
+    op("s", [a("su"), pick], [a("sS")], lambda: g.scalar.activation(T.sS[:], T.su[:].indirect(pick[0]), ACT.Copy))
+    ts(a("Mr"), a("j4", 0, 240), 0.0, ALU.is_equal, -16384.0, ALU.mult)
+    ts(a("nm4"), a("j4"), c3, ALU.not_equal)
+    act(aw, w5, ACT.Abs, 3.0, 1.0)
+    lin(a("io2"), a("I", 0, C), 2.0, -320.0)
+    act(pen, aw, ACT.Relu, -8192.0, 4096.0)
+    lin(a("TL", 0, L), a("I", 0, L), 1.0, 320.0)
+    lin(a("CX", 80, 160), pen, -1.0, -320.0)
+    lin(a("M4"), a("nm4"), K + BIG, -BIG)
+
+    PASS = {"A": 0, "B": 1, "C": 2}
+    BANK = {"A": 3, "B": 6, "C": 7}
+
+    def rows(x, row, key, m0, m1, w, base, sign=-1.0):
+        for m in range(m0, m1):
+            j = m - m0
+            o = a("t" + x, base + 4 * w * (j // 4) + j % 4, base + 4 * w * (j // 4 + 1), 4)
+            act(o, row(w), ACT.Sign, key(m), sign, c1("acc", 24 * PASS[x] + m))
+
+    def share(x, row, key, m0, m1):
+        for m in range(m0, m1):
+            ts(a("t" + x, TU + 512 * (m // 4) + m % 4, TU + 512 * (m // 4 + 1), 4), row(128), key(m), ALU.is_lt, 2.0, ALU.mult)
+
+    def cols(x, tile, q, w, start=False, stop=False):
+        quant(x, q, q + w, a("t" + x, tile, tile + 4 * w))
+        mm(BANK[x], "one", 0, x, q, q + w, start, stop)
+
+    def shared(x, j, stop=False):
+        cols(x, TU + 512 * j, QU + 128 * j, 128, False, stop)
+
+    def extract(x):
+        scan(a("ext", PASS[x] * C, PASS[x] * C + 256), a("M16", 0, 256), ps(BANK[x], 256), 0.0, ALU.add, ALU.max)
+
+    def lead(x):
+        j = PASS[x]
+        d = a("sm2", 20 * j, 20 * j + 20)
+        tt(d, a("ext", j * C + 15, (j + 1) * C, 16), a("acc", 24 * j, 24 * j + 20), ALU.subtract)
+        return d
+
+    def hold(lo, hi):
+        scan(a("sx", lo, hi), a("nmask", lo, hi), a("sm", lo, hi), 0.0, ALU.mult, ALU.add)
+
+    uS, uA, uB, uC, uP = a("ul", 0, 4), a("ul", 4, 24), a("ul", 24, 44), a("ul", 44, 64), a("ul", 64, 84)
+
+    for t in range(R):
+        tw, nx = "tw%d" % t, "tw%d" % (t + 1)
+        qT = "T%d" % t
+        quant(qT, 0, C, a(tw, 0, 4 * C))
+        mm(6, "S", 0, qT, 192, C)
+        mm(0, "S", 0, qT, 0, C)
+        mm(4, "S", 0, qT, 0, 192)
+        mm(1, "u", 0, qT, 0, C)
+        send(t, "q", a("q" + qT))
+        send(t, "s", a("s" + qT))
+        if t == 0:
+            iota(a("ones"), [[0, 512]], 1, 0)
+            for b in range(4):
+                o = a("E", 512 * b, 512 * b + 512)
+                op("g", [a("ones")], [o], lambda: g.affine_select(o[0], T.ones[:], [[-1, 512]], ALU.is_equal, 0.0, b, 4))
+            ts(a("one"), a("g8"), cg, ALU.is_equal)
+
+        rowA, rowA2, keyA = (lambda w: ps(0, w)), (lambda w: ps(4, w)), (lambda m: c1("sx", 16 * m + 15))
+        tt(a("sm", 192, C), ps(6, 128), a("mask", 0, 128), ALU.mult)
+        if t == 0:
+            quant("one", 0, 128, a("one"))
+        hold(192, C)
+        tt(a("sm", 0, 192), ps(4, 192), a("mask", 0, 192), ALU.mult)
+        ts(a("bits", 0, 4 * C, 4), ps(1), 0.0, ALU.is_gt, powc, ALU.mult)
+        hold(0, 192)
+        rows("A", rowA, keyA, 16, 20, 320, T4)
+        quant("bits", 0, C, a("bits"))
+        mm(2, "one", 0, "bits", 0, C)
+        mm(5, "one", 0, "bits", 0, C)
+        rows("A", rowA, keyA, 12, 16, 256, T3)
+        rows("A", rowA, keyA, 8, 12, 192, T2)
+        share("A", rowA2, keyA, 0, 4)
+        cols("A", T4, Q4, 256, start=True)
+        for j in range(4):
+            act(a("tB", j, 4 * C, 4), ps(2), ACT.Sign, c1("kw", 40 + j), 1.0, c1("acc", 20 + j))
+        if t == 0:
+            lin(a("krow"), a("I", 0, C), 511.0, 512.0)
+        shared("A", 0)
+        share("A", rowA2, keyA, 4, 8)
+        cols("A", T3, Q3, 192)
+        shared("A", 1)
+        scan(a("eh"), a("M16"), ps(5), 0.0, ALU.add, ALU.max)
+        tt(a("hk"), ps(5), a("crow"), ALU.add)
+        cols("A", T2, Q2, 128, stop=True)
+        extract("A")
+        dA = lead("A")
+        ts(uA, dA, colA, ALU.add)
+        tt(a("sm2", 60, 80), a("eh", 15, C, 16), dA, ALU.subtract)
+        tt(a("kB", 0, 128), ind(a("J"), a("ul", 4, 12)), a("hk", 0, 128), ALU.subtract)
+        tt(a("sm2", 80, 100), a("sm2", 60, 80), constw, ALU.add)
+        tt(a("kB", 128, C), ind(a("J"), a("ul", 12, 24)), a("hk", 128, C), ALU.subtract)
+        if t == 0:
+            tt(a("CX", 160, 240), cc, pen, ALU.subtract)
+            tt(a("CX", 0, 80), a("CX", 80, 160), w5, ALU.subtract)
+
+        rowB, keyB = (lambda w: a("kB", 0, w)), (lambda m: c1("sm2", 80 + m))
+        rows("B", rowB, keyB, 0, 8, 128, TU, 1.0)
+        rows("B", rowB, keyB, 16, 20, 320, T4, 1.0)
+        rows("B", rowB, keyB, 12, 16, 256, T3, 1.0)
+        rows("B", rowB, keyB, 8, 12, 192, T2, 1.0)
+        ts(uS, a("acc", 20, 24), 0.5, ALU.mult, 160.0, ALU.add)
+        ts(a("hs", 0, 4 * C, 4), a("io2"), c1("acc", 20), ALU.is_ge, -2560.0, ALU.mult)
+        tt(a("Z", 0, 64), ind(a("I"), uS), a("c64"), ALU.subtract)
+        ts(a("hs", 1, 4 * C, 4), a("io2"), c1("acc", 21), ALU.is_ge, -2560.0, ALU.mult)
+        scan(a("Z", 65, 129), a("Z", 0, 64), a("Z", 0, 64), 0.0, ALU.min, ALU.min)
+        ts(a("hs", 2, 4 * C, 4), a("io2"), c1("acc", 22), ALU.is_ge, -2560.0, ALU.mult)
+        ts(cfix, c1("Z", 128), m15, ALU.mult, c1("acc", 23), ALU.add)
+        tt(a("EX"), ind(a("Z", 0, 129), a("xl", 0, 15)), a("CX"), ALU.add)
+        ts(a("hs", 3, 4 * C, 4), a("io2"), cfix, ALU.is_ge, w3, ALU.mult)
+        scan(a("EY"), a("Mr"), a("EX"), 0.0, ALU.add, ALU.max)
+        quant("hs", 0, C, a("hs"))
+        mm(1, "one", 0, "hs", 0, C)
+        e2, e1, e3 = a("EY", 3, 80, 4), a("EY", 83, 160, 4), a("EY", 163, 240, 4)
+        fr, z, zf, pos = (a("sm2", 100 + 20 * j, 120 + 20 * j) for j in range(4))
+        tt(fr, e1, e2, ALU.is_ge)
+        ts(z, e2, c1("Z", 128), ALU.subtract, -1.0, ALU.mult)
+        tt(zf, z, fr, ALU.mult)
+        cp(a("X"), ps(1))
+        tt(pos, zf, e3, ALU.max)
+        cols("B", T4, Q4, 256, start=True)
+        cp(uP, pos)
+        tt(a("kC"), ind(a("X"), uP), a("krow"), ALU.add)
+        cols("B", T3, Q3, 192)
+        scan(a("eC"), a("M16"), a("kC"), 0.0, ALU.add, ALU.max)
+        ts(a("sm2", 180, 200), a("eC", 15, C, 16), K16, ALU.subtract)
+
+        rowC, keyC = (lambda w: a("kC", 0, w)), (lambda m: c1("sm2", 180 + m))
+        rows("C", rowC, keyC, 16, 20, 320, T4)
+        rows("C", rowC, keyC, 12, 16, 256, T3)
+        rows("C", rowC, keyC, 8, 12, 192, T2)
+        share("C", rowC, keyC, 0, 4)
+        cols("B", T2, Q2, 128, stop=True)
+        share("C", rowC, keyC, 4, 7)
+        extract("B")
+        share("C", rowC, keyC, 7, 8)
+        dB = lead("B")
+        share("C", rowC, keyC, 8, 9)
+        ts(uB, dB, 0.5, ALU.mult, colB, ALU.add)
+        share("C", rowC, keyC, 9, 12)
+        cols("C", T4, Q4, 256, start=True)
+        shared("C", 0)
+        shared("C", 1)
+        shared("C", 2)
+        cols("C", T3, Q3, 192, stop=True)
+        scatter(a("orow"), uB, a("I", 0, C))
+        act(a("mrow"), ind(a("orow"), uP), ACT.Copy)
+        extract("C")
+        dC = lead("C")
+        ts(uC, dC, 0.5, ALU.mult, colB, ALU.add)
+        scatter(a("brow"), uC, a("mrow"))
+        scan(a("eo", C, C + L), a("M4", 0, L), a("brow", 0, L), 0.0, ALU.add, ALU.max)
+        ts(a("sl%d" % t), a("eo", C + 3, C + L, 4), 4.0, ALU.mult, col4, ALU.add)
+        send(t, "l", a("sl%d" % t))
+
+        if t == 0:
+            quant("E", 0, 512, a("E"))
+        for b in range(4):
+            mm(4 + b, "E", 128 * b, "L%d" % t, 0, C)
+        for b in range(4):
+            act(a("D", b, 4 * C, 4), ps(4 + b), ACT.Copy)
+        tt(a("otr"), ind(a("TL"), uC), a("mrow"), ALU.max)
+        if t == 0:
+            quant("v", 0, 128, a("vb"))
+        scan(a("eo", 0, C), a("M4"), a("otr"), 0.0, ALU.add, ALU.max)
+        ts(a("off"), a("eo", 3, C, 4), 4.0, ALU.mult, col4, ALU.add)
+        if t == R - 1:
+            dma("y", T.ot[:], T.otr[0:128:16, :], [a("otr")], [], "dout")
+
+        ll = "ll%d" % t
+        cp(a(tw, 4 * C, 4 * C + 2 * L), ind(a("D"), a(ll, 0, 12)))
+        act(a(tw, 4 * C + 2 * L, 4 * C + 4 * L), ind(a("D"), a(ll, 12, 24)), ACT.Copy)
+        cp(a("V", 0, 2 * C), ind(a(tw), a("off", 0, 40)))
+        act(a("V", 2 * C, 4 * C), ind(a(tw), a("off", 40, 80)), ACT.Copy)
+        quant("V", 0, C, a("V"))
+        for b in range(4):
+            mm(4 + b, "w", 128 * b, "V", 0, C)
+        act(a("V64", 0, 4 * C, 4), a("V", 0, 4 * C, 4), ACT.Copy, None, 64.0)
+        act(a("V64", 2, 4 * C, 4), a("V", 2, 4 * C, 4), ACT.Copy, None, 64.0)
+        ts(a("V64", 1, 4 * C, 4), a("V", 1, 4 * C, 4), 64.0, ALU.mult)
+        for b in range(3):
+            tt(a("tmp", b * C, b * C + C), ps(4 + b), a("V64", b, 4 * C, 4), ALU.add)
+            act(a(nx, b, 4 * C, 4), a("tmp", b * C, b * C + C), ACT.Copy, None, 0.015625)
+            if b == 0:
+                act(a("tmp", 3 * C, 4 * C), ps(7), ACT.Copy, None, 0.015625)
+        tt(a(nx, 3, 4 * C, 4), a("tmp", 3 * C, 4 * C), a("V", 3, 4 * C, 4), ALU.add)
+
+    last = "T%d" % R
+    quant(last, 0, C, a("tw%d" % R, 0, 4 * C))
+    mm(0, "v", 0, last, 0, C)
+    dma("y", T.oc[:], T["q" + last][:].bitcast(dt.uint8), [a("q" + last)], [], "dout")
+    for k in range(4):
+        dma("s" if k % 2 else "y", T.osc[4 * k:4 * k + 4, :], T["s" + last][32 * k:32 * k + 4, :], [a("s" + last)], [], "dout")
+    cp(a("yb"), ps(0))
+    dma("s", T.y[:], T.yb[:], [a("yb")], [], "dout")
+    for sem in count:
+        g.wait_ge(T.sem[sem], count[sem])

@@ -34,12 +34,12 @@ for _n, _w in (("u", 128), ("S", 128), ("v", 128), ("w", 512), ("one", 128), ("E
                ("V", C), ("A", 960), ("B", 960), ("C", 960)):
     _pair(_n, _w)
 for _n, _w in (("ub", 512), ("vb", 512), ("j16", C), ("g8", 512), ("one", 512), ("ones", 512), ("E", 2048), ("j4", C),
-               ("mask", C), ("nmask", C), ("nm4", C), ("M16", C), ("M4", C), ("Mr", 240),
+               ("mask", C), ("nmask", C), ("nm4", C), ("M16", C), ("M4", C), ("Mr", 240), ("ab", 16),
                ("io2", C), ("bits", 4 * C), ("hs", 4 * C), ("tA", 4608), ("tB", 4608), ("tC", 4608),
                ("D", 4 * C), ("V", 4 * C), ("V64", 4 * C)):
     _sb(_n, _w, BF)
 for _n, _w in (("I", 328), ("J", 648), ("c80", 80), ("cf", 4), ("col", 24), ("pw", 24), ("kw", 48), ("crow", C), ("krow", C),
-               ("c64", 64), ("TL", C), ("cx", 400), ("CX", 240), ("sm", C), ("sx", C), ("eh", C), ("hk", C), ("acc", 72),
+               ("c64", 64), ("TL", C), ("cx", 400), ("CX", 240), ("sm", C), ("sx", C), ("hk", C), ("acc", 72),
                ("ext", 3 * C), ("Z", 136), ("EX", 240), ("EY", 240), ("sm2", 240), ("X", C), ("kB", C), ("kC", C), ("eC", C),
                ("orow", C), ("mrow", C), ("brow", C), ("otr", C), ("eo", C + L), ("tmp", 4 * C), ("yb", C)):
     _sb(_n, _w, F32)
@@ -237,17 +237,18 @@ def rank_program(g, core, T, topo):
     dma("y", T.vb[:], T.v[:], [], [a("vb")], "dv")
 
     c0, cg, c2, c3 = (c1("cf", j) for j in range(4))
-    (K16, c4a, col4, colA, colB, w3, m15, c820, powc, cfix) = (c1("col", j) for j in range(10))
+    (K16, c4a, col4, colB, m15, c820, powc) = (c1("col", j) for j in range(7))
+    w3, cfix = c1("ab", 8), c1("ab", 4)
     kwc, constw, thrb = a("kw", 0, 20), a("kw", 20, 40), a("kw", 40, 44)
     cc, h5, w5, aw, pen = (a("cx", 80 * j, 80 * j + 80) for j in range(5))
     iota(a("ip", 0, 1), [[0, 1]], 0, 1)
     iota(a("j16"), [[0, 20], [1, 16]])
     iota(a("ip", 8, 16), [[16, 8]], 8, 0)
+    iota(a("g8"), [[1, 8], [0, 64]])
     iota(a("I"), [[1, 328]])
     iota(a("c80"), [[16, 20], [0, 4]])
     iota(a("q5", 0, 5), [[64 * 205, 5]])
     iota(a("j4"), [[0, 80], [4, 4]])
-    iota(a("g8"), [[1, 8], [0, 64]])
     iota(a("J"), [[1, 648]])
     fill(a("bits"), 0.0)
     ts(c1("ip", 4), c1("ip", 0), 15, ALU.bitwise_and)
@@ -263,54 +264,51 @@ def rank_program(g, core, T, topo):
     lin(c820, c3, 820.0, 0.0)
     lin(K16, c0, -K, 15 * K)
     lin(c4a, c3, K, c2)
-    lin(w3, c1("mask", 15), 166400.0, -2560.0)
+    lin(w3, c1("mask", 15), 58240.0, -896.0)
     lin(m15, c1("mask", 15), 2.0, 0.0)
     lin(a("M16"), a("nmask"), K + BIG, -BIG)
-    lin(colA, K16, -1.0, 320.0)
     lin(colB, K16, -0.5, 159.5)
     lin(col4, c4a, 1.0, -12 * K)
     tt(a("pw", 16, 22), a("pw", 8, 14), a("mask", 0, 6), ALU.mult)
     fill(a("acc", 0, 8), 127.0)
     fill(a("acc", 48, 56), 191.0)
-    op("v", [a("pw", 16, 22)], [powc], lambda: g.vector.tensor_reduce(powc[0], a("pw", 16, 22)[0], AxisListType.X, ALU.add, negate=True))
+    op("v", [a("pw", 16, 22)], [powc], lambda: g.vector.tensor_reduce(powc[0], a("pw", 16, 22)[0], AxisListType.X, ALU.add))
     fill(c1("Z", 64), 0.0)
+    fill(a("tB", TU + 1024, TU + 1536), 0.0)
     fill(a("TL", L, C), 0.0)
-    lin(a("crow"), a("I", 0, C), -1.0 / 512, 20480.0)
+    lin(a("crow"), a("I", 0, C), 1.0 / 512, -19840.0)
     lin(kwc, a("c80", 0, 80, 4), 1.0, c0)
     lin(cc, a("c80"), 1.0, c0)
-    lin(a("c64"), a("I", 0, 64), 5.0, 5.0)
     lin(thrb, a("kw", 0, 4), 640.0, 320.0)
+    lin(a("CX", 160, 180), kwc, 1.0, 320.0)
     lin(constw, kwc, -1.0 / 512, 20160.0)
+    ts(a("one"), a("g8"), cg, ALU.is_equal)
+    quant("B", QU + 128, QU + 256, a("tB", TU + 1024, TU + 1536))
+    quant("one", 0, 128, a("one"))
+    quant("u", 0, 128, a("ub"))
+    pick = a("pk")
+    op("v", [a("qu"), pick], [a("qS")], lambda: g.vector.tensor_copy(T.qS[:].bitcast(dt.uint32), T.qu[:].bitcast(dt.uint32).indirect(pick[0])))
+    op("s", [a("su"), pick], [a("sS")], lambda: g.scalar.activation(T.sS[:], T.su[:].indirect(pick[0]), ACT.Copy))
     ts(a("q5", 8, 13), a("q5", 0, 5), c820, ALU.add)
     ts(a("q5", 8, 13), a("q5", 8, 13), 10, ALU.logical_shift_right)
     ts(a("xl", 0, 5), a("q5", 8, 13), c2, ALU.add)
     ts(a("xl", 5, 10), a("q5", 8, 13), c2, ALU.add, 64.0, ALU.add)
-    ts(a("xl", 10, 15), a("q5", 8, 13), c2, ALU.add, 64.0, ALU.add)
     ts(h5, ind(a("I", 0, 64), a("xl", 0, 5)), 5.0, ALU.mult, 5.0, ALU.add)
-    quant("u", 0, 128, a("ub"))
     tt(w5, cc, h5, ALU.subtract)
-    pick = a("pk")
-    op("v", [a("qu"), pick], [a("qS")], lambda: g.vector.tensor_copy(T.qS[:].bitcast(dt.uint32), T.qu[:].bitcast(dt.uint32).indirect(pick[0])))
-    for j in range(3):
+    for j in (1, 2):
         lin(a("ext", j * C + 256, (j + 1) * C), a("I", 0, 64), 0.0, K16)
-    op("s", [a("su"), pick], [a("sS")], lambda: g.scalar.activation(T.sS[:], T.su[:].indirect(pick[0]), ACT.Copy))
-    ts(a("Mr"), a("j4", 0, 240), 0.0, ALU.is_equal, -16384.0, ALU.mult)
-    ts(a("nm4"), a("j4"), c3, ALU.not_equal)
     act(aw, w5, ACT.Abs, 3.0, 1.0)
-    lin(a("io2"), a("I", 0, C), 2.0, -320.0)
     act(pen, aw, ACT.Relu, -8192.0, 4096.0)
-    lin(a("TL", 0, L), a("I", 0, L), 1.0, 320.0)
     lin(a("CX", 80, 160), pen, -1.0, -320.0)
-    lin(a("M4"), a("nm4"), K + BIG, -BIG)
 
     PASS = {"A": 0, "B": 1, "C": 2}
     BANK = {"A": 3, "B": 6, "C": 7}
 
-    def rows(x, row, key, m0, m1, w, base, sign=-1.0):
+    def rows(x, row, key, m0, m1, w, base):
         for m in range(m0, m1):
             j = m - m0
             o = a("t" + x, base + 4 * w * (j // 4) + j % 4, base + 4 * w * (j // 4 + 1), 4)
-            act(o, row(w), ACT.Sign, key(m), sign, c1("acc", 24 * PASS[x] + m))
+            act(o, row(w), ACT.Sign, key(m), -1.0, c1("acc", 24 * PASS[x] + m))
 
     def share(x, row, key, m0, m1):
         for m in range(m0, m1):
@@ -340,7 +338,8 @@ def rank_program(g, core, T, topo):
     for t in range(R):
         tw, nx = "tw%d" % t, "tw%d" % (t + 1)
         qT = "T%d" % t
-        quant(qT, 0, C, a(tw, 0, 4 * C))
+        quant(qT, 192, C, a(tw, 768, 4 * C))
+        quant(qT, 0, 192, a(tw, 0, 768))
         mm(6, "S", 0, qT, 192, C)
         mm(0, "S", 0, qT, 0, C)
         mm(4, "S", 0, qT, 0, 192)
@@ -348,16 +347,17 @@ def rank_program(g, core, T, topo):
         send(t, "q", a("q" + qT))
         send(t, "s", a("s" + qT))
         if t == 0:
+            iota(a("c64"), [[5, 64]], 5)
+            iota(a("io2"), [[2, C]], -320)
+            iota(a("krow"), [[179, C]], 64)
+            iota(a("TL", 0, L), [[1, L]], 320)
             iota(a("ones"), [[0, 512]], 1, 0)
             for b in range(4):
                 o = a("E", 512 * b, 512 * b + 512)
                 op("g", [a("ones")], [o], lambda: g.affine_select(o[0], T.ones[:], [[-1, 512]], ALU.is_equal, 0.0, b, 4))
-            ts(a("one"), a("g8"), cg, ALU.is_equal)
 
         rowA, rowA2, keyA = (lambda w: ps(0, w)), (lambda w: ps(4, w)), (lambda m: c1("sx", 16 * m + 15))
         tt(a("sm", 192, C), ps(6, 128), a("mask", 0, 128), ALU.mult)
-        if t == 0:
-            quant("one", 0, 128, a("one"))
         hold(192, C)
         tt(a("sm", 0, 192), ps(4, 192), a("mask", 0, 192), ALU.mult)
         ts(a("bits", 0, 4 * C, 4), ps(1), 0.0, ALU.is_gt, powc, ALU.mult)
@@ -365,63 +365,66 @@ def rank_program(g, core, T, topo):
         rows("A", rowA, keyA, 16, 20, 320, T4)
         quant("bits", 0, C, a("bits"))
         mm(2, "one", 0, "bits", 0, C)
-        mm(5, "one", 0, "bits", 0, C)
+        mm(3, "one", 0, "bits", 0, C, True, False)
         rows("A", rowA, keyA, 12, 16, 256, T3)
         rows("A", rowA, keyA, 8, 12, 192, T2)
         share("A", rowA2, keyA, 0, 4)
-        cols("A", T4, Q4, 256, start=True)
+        cols("A", T4, Q4, 256)
         for j in range(4):
-            act(a("tB", j, 4 * C, 4), ps(2), ACT.Sign, c1("kw", 40 + j), 1.0, c1("acc", 20 + j))
-        if t == 0:
-            lin(a("krow"), a("I", 0, C), 511.0, 512.0)
+            act(a("tB", j, 4 * C, 4), ps(2), ACT.Sign, c1("kw", 40 + j), -1.0, c1("acc", 20 + j))
         shared("A", 0)
         share("A", rowA2, keyA, 4, 8)
         cols("A", T3, Q3, 192)
         shared("A", 1)
-        scan(a("eh"), a("M16"), ps(5), 0.0, ALU.add, ALU.max)
-        tt(a("hk"), ps(5), a("crow"), ALU.add)
-        cols("A", T2, Q2, 128, stop=True)
-        extract("A")
-        dA = lead("A")
-        ts(uA, dA, colA, ALU.add)
-        tt(a("sm2", 60, 80), a("eh", 15, C, 16), dA, ALU.subtract)
-        tt(a("kB", 0, 128), ind(a("J"), a("ul", 4, 12)), a("hk", 0, 128), ALU.subtract)
-        tt(a("sm2", 80, 100), a("sm2", 60, 80), constw, ALU.add)
-        tt(a("kB", 128, C), ind(a("J"), a("ul", 12, 24)), a("hk", 128, C), ALU.subtract)
         if t == 0:
-            tt(a("CX", 160, 240), cc, pen, ALU.subtract)
+            ts(a("Mr"), a("j4", 0, 240), 0.0, ALU.is_equal, -16384.0, ALU.mult)
+            ts(a("nm4"), a("j4"), c3, ALU.not_equal)
             tt(a("CX", 0, 80), a("CX", 80, 160), w5, ALU.subtract)
+        cols("A", T2, Q2, 128, stop=True)
+        ts(uA, a("acc", 0, 20), 320.0, ALU.add)
+        tt(a("sm2", 0, 20), a("acc", 0, 20), constw, ALU.add)
+        scan(a("ext", 0, C), a("M16"), ps(3), 0.0, ALU.add, ALU.max)
+        tt(a("hk"), ps(3), a("crow"), ALU.add)
+        ts(a("sm2", 60, 80), a("ext", 15, C, 16), -1.0, ALU.mult, K16, ALU.add)
+        tt(a("kB", 0, 128), ind(a("J"), a("ul", 4, 12)), a("hk", 0, 128), ALU.subtract)
+        tt(a("sm2", 80, 100), a("sm2", 60, 80), a("sm2", 0, 20), ALU.add)
+        tt(a("kB", 128, C), ind(a("J"), a("ul", 12, 24)), a("hk", 128, C), ALU.subtract)
 
         rowB, keyB = (lambda w: a("kB", 0, w)), (lambda m: c1("sm2", 80 + m))
-        rows("B", rowB, keyB, 0, 8, 128, TU, 1.0)
-        rows("B", rowB, keyB, 16, 20, 320, T4, 1.0)
-        rows("B", rowB, keyB, 12, 16, 256, T3, 1.0)
-        rows("B", rowB, keyB, 8, 12, 192, T2, 1.0)
+        rows("B", rowB, keyB, 0, 4, 64, TU)
+        rows("B", rowB, keyB, 4, 8, 128, TU + 256)
+        rows("B", rowB, keyB, 16, 20, 320, T4)
+        cp(a("ab", 0, 3), a("acc", 20, 23))
         ts(uS, a("acc", 20, 24), 0.5, ALU.mult, 160.0, ALU.add)
-        ts(a("hs", 0, 4 * C, 4), a("io2"), c1("acc", 20), ALU.is_ge, -2560.0, ALU.mult)
+        ts(a("hs", 0, 4 * C, 4), a("io2"), c1("ab", 0), ALU.is_ge, -896.0, ALU.mult)
         tt(a("Z", 0, 64), ind(a("I"), uS), a("c64"), ALU.subtract)
-        ts(a("hs", 1, 4 * C, 4), a("io2"), c1("acc", 21), ALU.is_ge, -2560.0, ALU.mult)
+        ts(a("hs", 1, 4 * C, 4), a("io2"), c1("ab", 1), ALU.is_ge, -896.0, ALU.mult)
         scan(a("Z", 65, 129), a("Z", 0, 64), a("Z", 0, 64), 0.0, ALU.min, ALU.min)
-        ts(a("hs", 2, 4 * C, 4), a("io2"), c1("acc", 22), ALU.is_ge, -2560.0, ALU.mult)
+        ts(a("hs", 2, 4 * C, 4), a("io2"), c1("ab", 2), ALU.is_ge, -896.0, ALU.mult)
         ts(cfix, c1("Z", 128), m15, ALU.mult, c1("acc", 23), ALU.add)
-        tt(a("EX"), ind(a("Z", 0, 129), a("xl", 0, 15)), a("CX"), ALU.add)
+        tt(a("EX", 0, 160), ind(a("Z", 0, 129), a("xl", 0, 10)), a("CX", 0, 160), ALU.add)
         ts(a("hs", 3, 4 * C, 4), a("io2"), cfix, ALU.is_ge, w3, ALU.mult)
-        scan(a("EY"), a("Mr"), a("EX"), 0.0, ALU.add, ALU.max)
+        scan(a("EY", 0, 160), a("Mr", 0, 160), a("EX", 0, 160), 0.0, ALU.add, ALU.max)
         quant("hs", 0, C, a("hs"))
         mm(1, "one", 0, "hs", 0, C)
-        e2, e1, e3 = a("EY", 3, 80, 4), a("EY", 83, 160, 4), a("EY", 163, 240, 4)
+        act(a("X"), ps(1), ACT.Copy)
+        rows("B", rowB, keyB, 12, 16, 256, T3)
+        rows("B", rowB, keyB, 8, 12, 192, T2)
+        e2, e1, e3 = a("EY", 3, 80, 4), a("EY", 83, 160, 4), a("EY", 160, 180)
         fr, z, zf, pos = (a("sm2", 100 + 20 * j, 120 + 20 * j) for j in range(4))
         tt(fr, e1, e2, ALU.is_ge)
         ts(z, e2, c1("Z", 128), ALU.subtract, -1.0, ALU.mult)
+        tt(e3, e1, a("CX", 160, 180), ALU.add)
+        quant("B", QU, QU + 128, a("tB", TU, TU + 512))
         tt(zf, z, fr, ALU.mult)
-        cp(a("X"), ps(1))
         tt(pos, zf, e3, ALU.max)
         cols("B", T4, Q4, 256, start=True)
+        mm(BANK["B"], "one", 0, "B", QU + 64, QU + 192, False, False)
         cp(uP, pos)
         tt(a("kC"), ind(a("X"), uP), a("krow"), ALU.add)
-        cols("B", T3, Q3, 192)
         scan(a("eC"), a("M16"), a("kC"), 0.0, ALU.add, ALU.max)
         ts(a("sm2", 180, 200), a("eC", 15, C, 16), K16, ALU.subtract)
+        cols("B", T3, Q3, 192)
 
         rowC, keyC = (lambda w: a("kC", 0, w)), (lambda m: c1("sm2", 180 + m))
         rows("C", rowC, keyC, 16, 20, 320, T4)
@@ -443,6 +446,8 @@ def rank_program(g, core, T, topo):
         cols("C", T3, Q3, 192, stop=True)
         scatter(a("orow"), uB, a("I", 0, C))
         act(a("mrow"), ind(a("orow"), uP), ACT.Copy)
+        if t == 0:
+            lin(a("M4"), a("nm4"), K + BIG, -BIG)
         extract("C")
         dC = lead("C")
         ts(uC, dC, 0.5, ALU.mult, colB, ALU.add)
@@ -471,25 +476,27 @@ def rank_program(g, core, T, topo):
         cp(a("V", 0, 2 * C), ind(a(tw), a("off", 0, 40)))
         act(a("V", 2 * C, 4 * C), ind(a(tw), a("off", 40, 80)), ACT.Copy)
         quant("V", 0, C, a("V"))
-        for b in range(4):
+        for b in (0, 3, 1, 2):
             mm(4 + b, "w", 128 * b, "V", 0, C)
         act(a("V64", 0, 4 * C, 4), a("V", 0, 4 * C, 4), ACT.Copy, None, 64.0)
         act(a("V64", 2, 4 * C, 4), a("V", 2, 4 * C, 4), ACT.Copy, None, 64.0)
         ts(a("V64", 1, 4 * C, 4), a("V", 1, 4 * C, 4), 64.0, ALU.mult)
+        act(a("tmp", 3 * C, 4 * C), ps(7), ACT.Copy, None, 0.015625)
         for b in range(3):
             tt(a("tmp", b * C, b * C + C), ps(4 + b), a("V64", b, 4 * C, 4), ALU.add)
             act(a(nx, b, 4 * C, 4), a("tmp", b * C, b * C + C), ACT.Copy, None, 0.015625)
-            if b == 0:
-                act(a("tmp", 3 * C, 4 * C), ps(7), ACT.Copy, None, 0.015625)
         tt(a(nx, 3, 4 * C, 4), a("tmp", 3 * C, 4 * C), a("V", 3, 4 * C, 4), ALU.add)
 
     last = "T%d" % R
-    quant(last, 0, C, a("tw%d" % R, 0, 4 * C))
-    mm(0, "v", 0, last, 0, C)
+    quant(last, 0, 160, a("tw%d" % R, 0, 640))
+    quant(last, 160, C, a("tw%d" % R, 640, 4 * C))
+    mm(0, "v", 0, last, 0, 160)
+    mm(1, "v", 0, last, 160, C)
+    cp(a("yb", 0, 160), ps(0, 160))
+    act(a("yb", 160, C), ps(1, 160), ACT.Copy)
     dma("y", T.oc[:], T["q" + last][:].bitcast(dt.uint8), [a("q" + last)], [], "dout")
     for k in range(4):
-        dma("s" if k % 2 else "y", T.osc[4 * k:4 * k + 4, :], T["s" + last][32 * k:32 * k + 4, :], [a("s" + last)], [], "dout")
-    cp(a("yb"), ps(0))
+        dma("y", T.osc[4 * k:4 * k + 4, :], T["s" + last][32 * k:32 * k + 4, :], [a("s" + last)], [], "dout")
     dma("s", T.y[:], T.yb[:], [a("yb")], [], "dout")
     for sem in count:
         g.wait_ge(T.sem[sem], count[sem])

@@ -3,14 +3,16 @@ from concourse.mybir import dt, AluOpType, AxisListType, ActivationFunctionType
 ALU = AluOpType
 ACT = ActivationFunctionType
 C, L, R = 320, 96, 3
+H = 192
 STEP = [1, 2, 4]
 K = 262144.0
 BIG = 32 * K
 F32, BF, I32, U16, X4, U8 = "float32", "bfloat16", "int32", "uint16", "float8_e4m3fn_x4", "uint8"
-T4, T3, T2, TU = 0, 1280, 2304, 3072
-Q4, Q3, Q2, QU = 0, 256, 448, 576
+TILE = {4: (0, 0), 3: (1280, 256), 2: (2304, 448)}
+ONE, W320, PRE, SUF = 0, 128, 256, 384
 
 SCRATCH = {}
+PART = {}
 
 
 def _sb(name, n, d):
@@ -22,6 +24,14 @@ def _pair(name, n):
     _sb("s" + name, n, U8)
 
 
+def _parts(name, d, parts):
+    n = 0
+    for part, w in parts:
+        PART[part] = (name, n, w)
+        n += (w + 15) // 16 * 16
+    _sb(name, n, d)
+
+
 for _t in range(R + 1):
     _sb("tw%d" % _t, 4 * C + 4 * L, BF)
     _pair("T%d" % _t, C)
@@ -30,27 +40,32 @@ for _t in range(R):
     _pair("R%d" % _t, C)
     for _n in ("ll", "rl", "sl"):
         _sb("%s%d" % (_n, _t), 24, U16)
-for _n, _w in (("u", 128), ("S", 128), ("v", 128), ("w", 512), ("one", 128), ("E", 512), ("bits", C), ("hs", C),
-               ("V", C), ("A", 960), ("B", 960), ("C", 960)):
+for _n, _w in (("u", 128), ("S", 128), ("v", 128), ("w", 512), ("k", 512), ("E", 512), ("bits", C), ("hs", C),
+               ("V", C), ("A", 576), ("B", 576), ("U", 256), ("X", 2 * C)):
     _pair(_n, _w)
-for _n, _w in (("ub", 512), ("vb", 512), ("j16", C), ("g8", 512), ("one", 512), ("ones", 512), ("E", 2048), ("j4", C),
-               ("mask", C), ("nmask", C), ("nm4", C), ("M16", C), ("M4", C), ("Mr", 240), ("ab", 16),
-               ("io2", C), ("bits", 4 * C), ("hs", 4 * C), ("tA", 4608), ("tB", 4608), ("tC", 4608),
-               ("D", 4 * C), ("V", 4 * C), ("V64", 4 * C)):
+for _n, _w in (("ub", 512), ("vb", 512), ("kc", 2048), ("E", 2048), ("bits", 4 * C), ("hs", 4 * C), ("tA", 3072),
+               ("tB", 3072), ("tU", 768), ("t0", 256), ("tX", 4 * C + 16), ("io2", C + 32),
+               ("D", 4 * C), ("V", 4 * C), ("V64", 4 * C), ("tmp", 4 * C)):
     _sb(_n, _w, BF)
-for _n, _w in (("I", 328), ("J", 648), ("c80", 80), ("cf", 4), ("col", 24), ("pw", 24), ("kw", 48), ("crow", C), ("krow", C),
-               ("c64", 64), ("TL", C), ("cx", 400), ("CX", 240), ("sm", C), ("sx", C), ("hk", C), ("acc", 72),
-               ("ext", 3 * C), ("Z", 136), ("EX", 240), ("EY", 240), ("sm2", 240), ("X", C), ("kB", C), ("kC", C), ("eC", C),
-               ("orow", C), ("mrow", C), ("brow", C), ("otr", C), ("eo", C + L), ("tmp", 4 * C), ("yb", C)):
+for _n, _w in (("I", 2 * C), ("J", 640), ("TL", C), ("W", C + 8), ("Ms", 72), ("X", 2 * C), ("G", C), ("lp", C),
+               ("orow", C), ("otj", C), ("TLg", C), ("otr", C), ("yb", C)):
     _sb(_n, _w, F32)
-for _n, _w in (("ip", 16), ("q5", 16)):
+_parts("kb", BF, (("j16", C), ("g8", 512), ("j4", C), ("cb", 4), ("mask", C), ("nmask", C), ("nm4", C),
+                  ("M16", C), ("M8", C), ("M4", C), ("h68", 68), ("d4", 80), ("neg", 16)))
+_parts("kf", F32, (("cf", 4), ("col", 16), ("pw", 24), ("p8", 16), ("crow", C), ("cst", 48), ("cdm", 20), ("cz", 8),
+                   ("c64", 64), ("LV", C + 32), ("pr", C), ("px", C)))
+_parts("db", BF, (("ab", 4),))
+_parts("df", F32, (("sm", C), ("sx", C), ("hk", C), ("acc", 48), ("ext", 2 * C), ("z", 68), ("pre", 48), ("Y", 96),
+                   ("Yo", 80), ("dm", 20), ("TLn", C), ("sm2", 80), ("Xg", C), ("kB", C), ("kx", C), ("Gg", C),
+                   ("prow", C), ("es", 40), ("brow", L), ("eo", C + 2 * L)))
+for _n, _w in (("ip", 16), ("q5", 24)):
     _sb(_n, _w, I32)
-for _n, _w in (("pk", 8), ("xl", 16), ("ul", 88), ("off", 80)):
+for _n, _w in (("pk", 8), ("xl", 8), ("pm", 20), ("ul", 132), ("off", 80)):
     _sb(_n, _w, U16)
 for _b in range(8):
     SCRATCH["ps%d" % _b] = ("psum", [128, 512], F32)
 
-SEMAPHORES = ["ev", "es", "et", "eg", "dx", "du", "dw", "dv", "dout", "sent"] + \
+SEMAPHORES = ["ev", "es", "et", "eg", "dx", "dx2", "du", "dw", "dv", "dout", "sent"] + \
     ["%s%d" % (_n, _t) for _n in ("aq", "al") for _t in range(R)]
 
 
@@ -103,6 +118,9 @@ def rank_program(g, core, T, topo):
     log = {}
 
     def a(name, lo=0, hi=None, st=1):
+        if name in PART:
+            name, first, w = PART[name]
+            lo, hi = first + lo, first + (w if hi is None else hi)
         if hi is None:
             hi = SCRATCH[name][1][1]
         ap = T[name][:, lo:hi] if st == 1 else T[name][:, lo:hi:st]
@@ -172,7 +190,10 @@ def rank_program(g, core, T, topo):
         op("v", [in_, off], [win], lambda: g.vector.tensor_copy(win[0].indirect(off[0]), in_[0]))
 
     def scan(out, d0, d1, init, op0, op1):
-        op("v", [d0, d1], [out], lambda: g.vector.tensor_tensor_scan(out[0], d0[0], d1[0], init, op0, op1))
+        op("v", [d0, d1, init], [out], lambda: g.vector.tensor_tensor_scan(out[0], d0[0], d1[0], p(init), op0, op1))
+
+    def reduce(out, in_, o):
+        op("v", [in_], [out], lambda: g.vector.tensor_reduce(out[0], in_[0], AxisListType.X, o))
 
     def fill(out, v):
         op("v", [], [out], lambda: g.vector.memset(out[0], v))
@@ -197,19 +218,25 @@ def rank_program(g, core, T, topo):
     def lin(out, in_, scale, bias):
         act(out, in_, ACT.Identity, bias, scale)
 
+    def scp(out, in_, scale=1.0):
+        act(out, in_, ACT.Copy, None, scale)
+
     def iota(out, pattern, base=0, cm=0):
         if SCRATCH[out[1][0][0]][2] == I32:
             op("g", [], [out], lambda: g.iota(out[0], pattern, base, cm))
         else:
             op("g", [], [out], lambda: g.iota(out[0], pattern, base, cm, allow_small_or_imprecise_dtypes=True))
 
+    def select(out, in_, pattern, o, base, cm):
+        op("g", [in_], [out], lambda: g.affine_select(out[0], in_[0], pattern, o, 0.0, base, cm))
+
     def dma(e, out, in_, reads, writes, sem):
         order(e, reads, writes)
         Q[e].dma_start(out, in_).then_inc(T.sem[sem], 16)
         note(e, reads, writes, sem, 16)
 
-    def ps(b, w=C):
-        return a("ps%d" % b, 0, w)
+    def ps(b, lo=0, hi=C):
+        return a("ps%d" % b, lo, hi)
 
     def send(t, what, src):
         way = _route(core, T.cores[(rank + STEP[t]) % n], topo)
@@ -230,270 +257,388 @@ def rank_program(g, core, T, topo):
         note("far", [], [a("qL%d" % t), a("sL%d" % t)], "aq%d" % t, 2 * e)
         note("far", [], [a("ll%d" % t)], "al%d" % t, e)
 
-    dma("y", a("tw0", 0, 4 * C)[0], T.x[:], [], [a("tw0", 0, 4 * C)], "dx")
     dma("s", T.ub[:], T.u[:], [], [a("ub")], "du")
-    dma("y", T.qw[:].bitcast(dt.uint8), T.wc[:], [a("tw0", 0, 8)], [], "dw")
+    dma("y", a("tw0", 0, 4 * H)[0], T.x[:, 0:4 * H], [], [a("tw0", 0, 4 * H)], "dx")
+    dma("y", a("tw0", 4 * H, 4 * C)[0], T.x[:, 4 * H:4 * C], [], [a("tw0", 4 * H, 4 * C)], "dx2")
+    dma("y", T.qw[:].bitcast(dt.uint8), T.wc[:], [a("tw0", 4 * H, 4 * H + 8)], [], "dw")
     dma("y", T.sw[:], T.ws[:], [], [a("qw"), a("sw")], "dw")
     dma("y", T.vb[:], T.v[:], [], [a("vb")], "dv")
 
-    c0, cg, c2, c3 = (c1("cf", j) for j in range(4))
-    (K16, c4a, col4, colB, m15, c820, powc) = (c1("col", j) for j in range(7))
-    w3, cfix = c1("ab", 8), c1("ab", 4)
-    kwc, constw, thrb = a("kw", 0, 20), a("kw", 20, 40), a("kw", 40, 44)
-    cc, h5, w5, aw, pen = (a("cx", 80 * j, 80 * j + 80) for j in range(5))
+    c0, c2, c3 = c1("cf", 0), c1("cf", 2), c1("cf", 3)
+    b0, bg, b3 = c1("cb", 0), c1("cb", 1), c1("cb", 3)
+    K16, c4a, col4, colB, powc, thr0, cz0, c40, c40k, cLV, cy, off16, q103, odd4 = (c1("col", j) for j in range(14))
+    f8 = c1("p8", 15)
     iota(a("ip", 0, 1), [[0, 1]], 0, 1)
     iota(a("j16"), [[0, 20], [1, 16]])
     iota(a("ip", 8, 16), [[16, 8]], 8, 0)
+    iota(a("I", 0, C), [[1, C]])
     iota(a("g8"), [[1, 8], [0, 64]])
-    iota(a("I"), [[1, 328]])
-    iota(a("c80"), [[16, 20], [0, 4]])
-    iota(a("q5", 0, 5), [[64 * 205, 5]])
-    iota(a("j4"), [[0, 80], [4, 4]])
-    iota(a("J"), [[1, 648]])
-    fill(a("bits"), 0.0)
+    iota(a("q5", 0, 3), [[16 * 103, 3]])
+    iota(a("io2"), [[2, C + 32]], -320)
+    iota(a("c64"), [[10, 4], [40, 16]], -310)
+    fill(a("pw", 0, 6), 2.0)
+    fill(a("d4"), 0.0)
+    fill(a("h68", 64, 68), 0.0)
+    fill(a("neg"), -1.0)
     ts(c1("ip", 4), c1("ip", 0), 15, ALU.bitwise_and)
     ts(c1("ip", 5), c1("ip", 0), 4, ALU.logical_shift_right)
     ts(c1("ip", 6), c1("ip", 0), 3, ALU.bitwise_and)
     ts(c1("ip", 7), c1("ip", 0), 12, ALU.bitwise_and)
-    fill(a("pw", 0, 6), 2.0)
-    cp(a("cf"), a("ip", 4, 8))
+    ts(c1("q5", 20), c1("ip", 0), 1, ALU.bitwise_and)
     scan(a("pw", 8, 14), a("pw", 0, 6), a("pw", 0, 6), 320.0, ALU.mult, ALU.max)
+    fill(a("d4", 1, 80, 4), -4096.0)
+    fill(a("d4", 2, 80, 4), -1.0)
+    cp(a("cf"), a("ip", 4, 8))
+    cp(a("cb"), a("ip", 4, 8))
+    fill(a("bits"), 0.0)
+    ts(a("mask"), a("j16"), b0, ALU.is_equal)
+    ts(a("nmask"), a("j16"), b0, ALU.not_equal)
     cp(a("pk"), a("ip", 8, 16))
-    ts(a("mask"), a("j16"), c0, ALU.is_equal)
-    ts(a("nmask"), a("j16"), c0, ALU.not_equal)
-    lin(c820, c3, 820.0, 0.0)
-    lin(K16, c0, -K, 15 * K)
-    lin(c4a, c3, K, c2)
-    lin(w3, c1("mask", 15), 58240.0, -896.0)
-    lin(m15, c1("mask", 15), 2.0, 0.0)
-    lin(a("M16"), a("nmask"), K + BIG, -BIG)
-    lin(colB, K16, -0.5, 159.5)
-    lin(col4, c4a, 1.0, -12 * K)
+    fill(a("tU", 0, 256), 0.0)
     tt(a("pw", 16, 22), a("pw", 8, 14), a("mask", 0, 6), ALU.mult)
-    fill(a("acc", 0, 8), 127.0)
-    fill(a("acc", 48, 56), 191.0)
-    op("v", [a("pw", 16, 22)], [powc], lambda: g.vector.tensor_reduce(powc[0], a("pw", 16, 22)[0], AxisListType.X, ALU.add))
-    fill(c1("Z", 64), 0.0)
-    fill(a("tB", TU + 1024, TU + 1536), 0.0)
-    fill(a("TL", L, C), 0.0)
-    lin(a("crow"), a("I", 0, C), 1.0 / 512, -19840.0)
-    lin(kwc, a("c80", 0, 80, 4), 1.0, c0)
-    lin(cc, a("c80"), 1.0, c0)
-    lin(thrb, a("kw", 0, 4), 640.0, 320.0)
-    lin(a("CX", 160, 180), kwc, 1.0, 320.0)
-    lin(constw, kwc, -1.0 / 512, 20160.0)
-    ts(a("one"), a("g8"), cg, ALU.is_equal)
-    quant("B", QU + 128, QU + 256, a("tB", TU + 1024, TU + 1536))
-    quant("one", 0, 128, a("one"))
+    ts(a("M8"), a("nmask"), 8.0, ALU.mult)
+    ts(a("h68", 0, 64), a("j16", 0, 64), b0, ALU.is_ge, -1024.0, ALU.mult)
+    quant("U", 128, 256, a("bits", 0, 512))
+    reduce(powc, a("pw", 16, 22), ALU.add)
+    for x in (a("W", C, C + 8), a("Ms"), a("Y"), a("z", 64, 68), a("tX", 0, 16), a("es", 0, 5)):
+        fill(x, 0.0)
+    ts(odd4, c1("q5", 20), 4.0, ALU.mult)
+    scan(a("p8"), a("M8", 0, 16), a("neg"), 0.0, ALU.mult, ALU.min)
+    ts(a("kc", 512, 1024), a("g8"), bg, ALU.is_equal, 320.0, ALU.mult)
+    for col, scale, bias in ((q103, 103.0, 0.0), (off16, -1024.0, 16384.0), (thr0, 4 * 204800.0, 102400.0), (K16, -K, 15 * K),
+                             (cz0, 40.0, -310.0), (c40, 40.0, -319.0), (cy, 40.0, 0.0), (c40k, K - 40.0, 318.0 - 15 * K),
+                             (cLV, 40.0 - K, 15 * K - 318.0), (colB, -K / 2, 7.5 * K + 159.5)):
+        lin(col, c0, scale, bias)
+    lin(c4a, c3, K, c2)
+    lin(a("M16"), a("nmask"), K + BIG, -BIG)
+    lin(col4, c4a, 1.0, -12 * K)
+    lin(a("cz", 0, 4), a("I", 0, 4), 204800.0, thr0)
+    lin(a("cz", 4, 8), a("I", 0, 4), 10.0, cz0)
+    lin(a("cst", 0, 48, 2), a("I", 0, 24), 2.0, c40)
+    lin(a("cst", 1, 48, 2), a("I", 0, 24), 2.0, cy)
+    lin(a("cdm"), a("I", 0, 20), -2.0, c40k)
+    lin(a("ext", 256 + 15, C, 16), a("I", 0, 4), 0.0, K16)
+    lin(a("crow"), a("I", 0, C), 1.0, 2301632.0)
+    lin(a("J", 0, C), a("I", 0, C), -320.0, 0.0)
     quant("u", 0, 128, a("ub"))
+    ts(a("h68", 16, 68, 16), a("h68", 16, 68, 16), off16, ALU.add)
+    quant("k", W320, W320 + 128, a("kc", 512, 1024))
+    ts(a("q5", 8, 11), a("q5", 0, 3), q103, ALU.add)
     pick = a("pk")
     op("v", [a("qu"), pick], [a("qS")], lambda: g.vector.tensor_copy(T.qS[:].bitcast(dt.uint32), T.qu[:].bitcast(dt.uint32).indirect(pick[0])))
     op("s", [a("su"), pick], [a("sS")], lambda: g.scalar.activation(T.sS[:], T.su[:].indirect(pick[0]), ACT.Copy))
-    ts(a("q5", 8, 13), a("q5", 0, 5), c820, ALU.add)
-    ts(a("q5", 8, 13), a("q5", 8, 13), 10, ALU.logical_shift_right)
-    ts(a("xl", 0, 5), a("q5", 8, 13), c2, ALU.add)
-    ts(a("xl", 5, 10), a("q5", 8, 13), c2, ALU.add, 64.0, ALU.add)
-    ts(h5, ind(a("I", 0, 64), a("xl", 0, 5)), 5.0, ALU.mult, 5.0, ALU.add)
-    tt(w5, cc, h5, ALU.subtract)
-    for j in (1, 2):
-        lin(a("ext", j * C + 256, (j + 1) * C), a("I", 0, 64), 0.0, K16)
-    act(aw, w5, ACT.Abs, 3.0, 1.0)
-    act(pen, aw, ACT.Relu, -8192.0, 4096.0)
-    lin(a("CX", 80, 160), pen, -1.0, -320.0)
+    lin(a("kc", 0, 512), a("kc", 512, 1024), 1.0 / 320, 0.0)
+    lin(a("J", C, 2 * C), a("I", 0, C), -320.0, -102400.0)
+    lin(a("LV"), a("io2"), 1.0, cLV)
+    scp(a("I", C, 2 * C), a("I", 0, C))
+    lin(a("TL", 0, L), a("I", 0, L), 1.0, 320.0)
+    lin(a("TL", L, C), a("I", L, C), 0.0, 0.0)
+    ts(a("q5", 16, 19), a("q5", 8, 11), 10, ALU.logical_shift_right)
+    select(a("kc", 1024, 1536), a("kc", 0, 512), [[1, 128], [0, 4]], ALU.is_gt, 0, -1)
+    select(a("kc", 1536, 2048), a("kc", 0, 512), [[-1, 128], [0, 4]], ALU.is_ge, 0, 1)
 
-    PASS = {"A": 0, "B": 1, "C": 2}
-    BANK = {"A": 3, "B": 6, "C": 7}
+    def later_constants(step):
+        if step == 1:
+            ts(a("xl", 4, 7), a("q5", 16, 19), 3.0, ALU.min, 64.0, ALU.add)
+            ts(a("xl", 0, 3), a("q5", 16, 19), 3.0, ALU.min, odd4, ALU.max)
+            quant("k", ONE, ONE + 128, a("kc", 0, 512))
+        if step == 2:
+            for b in range(4):
+                select(a("E", 512 * b, 512 * b + 512), a("kc", 0, 512), [[-1, 512]], ALU.is_equal, b, 4)
+            iota(a("j4"), [[0, 80], [4, 4]])
+            iota(a("pr"), [[1, 16], [16, 20]])
+        if step == 3:
+            quant("k", PRE, PRE + 256, a("kc", 1024, 2048))
+        if step == 4:
+            ts(a("nm4"), a("j4"), b3, ALU.not_equal)
+            lin(a("M4"), a("nm4"), K + BIG, -BIG)
 
-    def rows(x, row, key, m0, m1, w, base):
-        for m in range(m0, m1):
-            j = m - m0
-            o = a("t" + x, base + 4 * w * (j // 4) + j % 4, base + 4 * w * (j // 4 + 1), 4)
-            act(o, row(w), ACT.Sign, key(m), -1.0, c1("acc", 24 * PASS[x] + m))
+    ACC = {"A": 0, "B": 24}
+    BANK = {"A": 3, "B": 6}
+    STAT = {"A": W320, "B": ONE}
 
-    def share(x, row, key, m0, m1):
-        for m in range(m0, m1):
-            ts(a("t" + x, TU + 512 * (m // 4) + m % 4, TU + 512 * (m // 4 + 1), 4), row(128), key(m), ALU.is_lt, 2.0, ALU.mult)
+    def rows(x, k):
+        w = 64 * (k + 1)
+        for j in range(4):
+            if k == 0:
+                o = a("t0", j, 256, 4)
+            elif k == 1:
+                o = a("tU", 256 + j, 256 + 4 * w, 4)
+            else:
+                o = a("t" + x, TILE[k][0] + j, TILE[k][0] + 4 * w, 4)
+            m = 4 * k + j
+            if x == "A":
+                act(o, ps(5 if w <= H else 0, 0, w), ACT.Sign, c1("sx", 16 * m + 15), -1.0, c1("acc", m))
+            else:
+                act(o, a("kB", 0, w), ACT.Sign, c1("kx", 16 * m + 15), f8, c1("acc", ACC[x] + m))
 
-    def cols(x, tile, q, w, start=False, stop=False):
-        quant(x, q, q + w, a("t" + x, tile, tile + 4 * w))
-        mm(BANK[x], "one", 0, x, q, q + w, start, stop)
+    def pack(x, k):
+        if k == 1:
+            quant("U", 0, 128, a("tU", 0, 512))
+        else:
+            quant(x, TILE[k][1], TILE[k][1] + 64 * k, a("t" + x, TILE[k][0], TILE[k][0] + 256 * k))
 
-    def shared(x, j, stop=False):
-        cols(x, TU + 512 * j, QU + 128 * j, 128, False, stop)
+    def cols(x, k, start=False, stop=False):
+        if k == 1:
+            mm(BANK[x], "k", STAT[x], "U", 64, 192, start, stop)
+            return
+        if k == 4:
+            mm(4, "k", STAT[x], x, 128, 256, start, True)
+        mm(BANK[x], "k", STAT[x], x, TILE[k][1], TILE[k][1] + min(64 * k, 192), start, stop)
 
-    def extract(x):
-        scan(a("ext", PASS[x] * C, PASS[x] * C + 256), a("M16", 0, 256), ps(BANK[x], 256), 0.0, ALU.add, ALU.max)
+    def wrap(out, row, lo, hi):
+        scan(a(out, lo, hi), a("M16", 0, hi - lo), row, 0.0, ALU.add, ALU.max)
 
-    def lead(x):
-        j = PASS[x]
-        d = a("sm2", 20 * j, 20 * j + 20)
-        tt(d, a("ext", j * C + 15, (j + 1) * C, 16), a("acc", 24 * j, 24 * j + 20), ALU.subtract)
-        return d
+    def keysA(bank, lo, hi, step):
+        if step == 0:
+            tt(a("sm", lo, hi), ps(bank, 0, hi - lo), a("mask", 0, hi - lo), ALU.mult)
+        else:
+            scan(a("sx", lo, hi), a("nmask", 0, hi - lo), a("sm", lo, hi), 0.0, ALU.mult, ALU.add)
 
-    def hold(lo, hi):
-        scan(a("sx", lo, hi), a("nmask", lo, hi), a("sm", lo, hi), 0.0, ALU.mult, ALU.add)
+    def keysB(lo, hi, step):
+        at = (lo + 128) % C
+        u, part, row = a("ul", lo // 16, hi // 16), a("hk", at, at + hi - lo), a("kB", at, at + hi - lo)
+        if step == 0:
+            ts(u, a("acc", lo // 16, hi // 16), 320.0, ALU.add)
+        elif step == 1:
+            tt(part, ind(a("J"), u), a("crow", lo, hi), ALU.add)
+        elif step == 2:
+            tt(row, ps(4, lo - 128, hi - 128) if lo else ps(3, lo, hi), part, ALU.add)
+        else:
+            scan(a("kx", at, at + hi - lo), a("M8", 0, hi - lo), row, 0.0, ALU.mult, ALU.max)
 
-    uS, uA, uB, uC, uP = a("ul", 0, 4), a("ul", 4, 24), a("ul", 24, 44), a("ul", 44, 64), a("ul", 64, 84)
+    def positions(lo, hi, step):
+        d, u = a("sm2", lo // 16, hi // 16), a("ul", 20 + lo // 16, 20 + hi // 16)
+        if step == 0:
+            tt(d, a("acc", 24 + lo // 16, 24 + hi // 16), a("ext", lo + 15, hi, 16), ALU.subtract)
+        elif step == 1:
+            ts(u, d, 0.5, ALU.mult, colB, ALU.add)
+        else:
+            scatter(a("orow"), u, a("I", 192 + lo, 192 + hi))
 
+    def w(lo, hi=None):
+        return a("W", C + lo, C + (lo + 1 if hi is None else hi))
+
+    def above(j):
+        ts(a("hs", j, 4 * C, 4), a("io2", 0, C), c1("ab", j), ALU.is_ge, 10.0, ALU.mult)
+
+    def same(out, k):
+        tt(out, a("dm", 5 * k, 20), a("dm", 0, 20 - 5 * k), ALU.is_equal)
+
+    def bits(bank, lo, hi):
+        ts(a("bits", 4 * lo, 4 * hi, 4), ps(bank, 0, hi - lo), 0.0, ALU.is_gt, powc, ALU.mult)
+
+    def add(bank, lo, hi, b):
+        tt(a("tmp", 4 * lo + b, 4 * hi, 4), ps(bank + b, 0, hi - lo), a("V64", 4 * lo + b, 4 * hi, 4), ALU.add)
+
+    def unpack(t):
+        for b, bank in enumerate((2, 3, 5, 7)):
+            mm(bank, "E", 128 * b, "L%d" % t, 0, C)
+        for b, bank in enumerate((2, 3, 5, 7)):
+            scp(a("D", b, 4 * C, 4), ps(bank))
+
+    def new_state(t):
+        tw, nx, ll = "tw%d" % t, "tw%d" % (t + 1), "ll%d" % t
+
+        def down(lo, hi, b):
+            if b < 3:
+                scp(a(nx, 4 * lo + b, 4 * hi, 4), a("tmp", 4 * lo + b, 4 * hi, 4), 0.015625)
+            else:
+                ts(a(nx, 4 * lo + b, 4 * hi, 4), a("tmp", 4 * lo + b, 4 * hi, 4), 0.015625, ALU.mult)
+
+        cp(a(tw, 4 * C, 4 * C + 2 * L), ind(a("D"), a(ll, 0, 12)))
+        scp(a(tw, 4 * C + 2 * L, 4 * C + 4 * L), ind(a("D"), a(ll, 12, 24)))
+        scp(a("V", 448, 4 * H), ind(a(tw), a("off", 28, 48)))
+        cp(a("V", 0, 448), ind(a(tw), a("off", 0, 28)))
+        scp(a("V", 4 * H, 4 * C), ind(a(tw), a("off", 48, 80)))
+        quant("V", 0, H, a("V", 0, 4 * H))
+        ts(a("V64", 0, 4 * H), a("V", 0, 4 * H), 64.0, ALU.mult)
+        for b in range(4):
+            mm(4 + b, "w", 128 * b, "V", 0, H)
+        quant("V", H, C, a("V", 4 * H, 4 * C))
+        scp(a("V64", 4 * H, 4 * C), a("V", 4 * H, 4 * C), 64.0)
+        for b in range(4):
+            mm(b, "w", 128 * b, "V", H, C)
+        for b in range(4):
+            add(4, 0, H, b)
+            if b < 3:
+                down(0, H, b)
+        add(0, H, C, 0)
+        add(0, H, C, 1)
+        down(0, H, 3)
+        add(0, H, C, 2)
+        add(0, H, C, 3)
+        for b in range(3):
+            down(H, C, b)
+        quant("T%d" % (t + 1), 0, H, a(nx, 0, 4 * H))
+        down(H, C, 3)
+
+    uC, uP, uD, uL, uS, uQ = (a("ul", lo, hi) for lo, hi in ((40, 60), (60, 80), (80, 100), (100, 106), (106, 110), (110, 130)))
+    zeros = a("bits", 1, 4 * C, 4)
+    cnt, red, pos2 = w(0, 4), c1("es", 36), a("Yo", 2, 80, 4)
+
+    quant("T0", 0, H, a("tw0", 0, 4 * H))
     for t in range(R):
-        tw, nx = "tw%d" % t, "tw%d" % (t + 1)
-        qT = "T%d" % t
-        quant(qT, 192, C, a(tw, 768, 4 * C))
-        quant(qT, 0, 192, a(tw, 0, 768))
-        mm(6, "S", 0, qT, 192, C)
-        mm(0, "S", 0, qT, 0, C)
-        mm(4, "S", 0, qT, 0, 192)
-        mm(1, "u", 0, qT, 0, C)
+        tw, qT = "tw%d" % t, "T%d" % t
+        first = t == 0
+
+        mm(6, "S", 0, qT, 0, H)
+        mm(7, "u", 0, qT, 0, H)
+        mm(5, "S", 0, qT, 0, H)
+        if first:
+            later_constants(1)
+        quant(qT, H, C, a(tw, 4 * H, 4 * C))
+        mm(1, "u", 0, qT, H, C)
+        mm(4, "S", 0, qT, H, C)
         send(t, "q", a("q" + qT))
         send(t, "s", a("s" + qT))
-        if t == 0:
-            iota(a("c64"), [[5, 64]], 5)
-            iota(a("io2"), [[2, C]], -320)
-            iota(a("krow"), [[179, C]], 64)
-            iota(a("TL", 0, L), [[1, L]], 320)
-            iota(a("ones"), [[0, 512]], 1, 0)
-            for b in range(4):
-                o = a("E", 512 * b, 512 * b + 512)
-                op("g", [a("ones")], [o], lambda: g.affine_select(o[0], T.ones[:], [[-1, 512]], ALU.is_equal, 0.0, b, 4))
+        if first:
+            later_constants(2)
+        keysA(6, 0, H, 0)
+        bits(7, 0, H)
+        keysA(6, 0, H, 1)
+        bits(1, H, C)
+        quant("bits", 0, H, a("bits", 0, 4 * H))
+        rows("A", 0)
+        rows("A", 1)
+        quant("bits", H, C, a("bits", 4 * H, 4 * C))
+        keysA(4, H, C, 0)
+        mm(2, "k", W320, "bits", 0, C)
+        mm(7, "k", W320, "bits", 0, C)
+        mm(0, "S", 0, qT, 0, C)
+        mm(3, "k", W320, "bits", 0, 192, True, False)
+        keysA(4, H, C, 1)
+        for j in range(1, 4):
+            act(a("tB", j, 4 * C, 4), ps(2), ACT.Sign, c1("cz", j), -1.0, w(j))
+        ts(a("tB", 0, 4 * C, 4), ps(7), c1("cz", 0), ALU.is_le, 2.0, ALU.mult)
+        pack("A", 1)
+        cols("A", 1)
+        mm(4, "k", W320, "bits", 128, C, True, False)
+        scan(a("W", 1, C + 1), a("tB", 0, 4 * C, 4), zeros, -320.0, ALU.add, ALU.add)
+        rows("A", 4)
 
-        rowA, rowA2, keyA = (lambda w: ps(0, w)), (lambda w: ps(4, w)), (lambda m: c1("sx", 16 * m + 15))
-        tt(a("sm", 192, C), ps(6, 128), a("mask", 0, 128), ALU.mult)
-        hold(192, C)
-        tt(a("sm", 0, 192), ps(4, 192), a("mask", 0, 192), ALU.mult)
-        ts(a("bits", 0, 4 * C, 4), ps(1), 0.0, ALU.is_gt, powc, ALU.mult)
-        hold(0, 192)
-        rows("A", rowA, keyA, 16, 20, 320, T4)
-        quant("bits", 0, C, a("bits"))
-        mm(2, "one", 0, "bits", 0, C)
-        mm(3, "one", 0, "bits", 0, C, True, False)
-        rows("A", rowA, keyA, 12, 16, 256, T3)
-        rows("A", rowA, keyA, 8, 12, 192, T2)
-        share("A", rowA2, keyA, 0, 4)
-        cols("A", T4, Q4, 256)
-        for j in range(4):
-            act(a("tB", j, 4 * C, 4), ps(2), ACT.Sign, c1("kw", 40 + j), -1.0, c1("acc", 20 + j))
-        shared("A", 0)
-        share("A", rowA2, keyA, 4, 8)
-        cols("A", T3, Q3, 192)
-        shared("A", 1)
-        if t == 0:
-            ts(a("Mr"), a("j4", 0, 240), 0.0, ALU.is_equal, -16384.0, ALU.mult)
-            ts(a("nm4"), a("j4"), c3, ALU.not_equal)
-            tt(a("CX", 0, 80), a("CX", 80, 160), w5, ALU.subtract)
-        cols("A", T2, Q2, 128, stop=True)
-        ts(uA, a("acc", 0, 20), 320.0, ALU.add)
-        tt(a("sm2", 0, 20), a("acc", 0, 20), constw, ALU.add)
-        scan(a("ext", 0, C), a("M16"), ps(3), 0.0, ALU.add, ALU.max)
-        tt(a("hk"), ps(3), a("crow"), ALU.add)
-        ts(a("sm2", 60, 80), a("ext", 15, C, 16), -1.0, ALU.mult, K16, ALU.add)
-        tt(a("kB", 0, 128), ind(a("J"), a("ul", 4, 12)), a("hk", 0, 128), ALU.subtract)
-        tt(a("sm2", 80, 100), a("sm2", 60, 80), a("sm2", 0, 20), ALU.add)
-        tt(a("kB", 128, C), ind(a("J"), a("ul", 12, 24)), a("hk", 128, C), ALU.subtract)
-
-        rowB, keyB = (lambda w: a("kB", 0, w)), (lambda m: c1("sm2", 80 + m))
-        rows("B", rowB, keyB, 0, 4, 64, TU)
-        rows("B", rowB, keyB, 4, 8, 128, TU + 256)
-        rows("B", rowB, keyB, 16, 20, 320, T4)
-        cp(a("ab", 0, 3), a("acc", 20, 23))
-        ts(uS, a("acc", 20, 24), 0.5, ALU.mult, 160.0, ALU.add)
-        ts(a("hs", 0, 4 * C, 4), a("io2"), c1("ab", 0), ALU.is_ge, -896.0, ALU.mult)
-        tt(a("Z", 0, 64), ind(a("I"), uS), a("c64"), ALU.subtract)
-        ts(a("hs", 1, 4 * C, 4), a("io2"), c1("ab", 1), ALU.is_ge, -896.0, ALU.mult)
-        scan(a("Z", 65, 129), a("Z", 0, 64), a("Z", 0, 64), 0.0, ALU.min, ALU.min)
-        ts(a("hs", 2, 4 * C, 4), a("io2"), c1("ab", 2), ALU.is_ge, -896.0, ALU.mult)
-        ts(cfix, c1("Z", 128), m15, ALU.mult, c1("acc", 23), ALU.add)
-        tt(a("EX", 0, 160), ind(a("Z", 0, 129), a("xl", 0, 10)), a("CX", 0, 160), ALU.add)
-        ts(a("hs", 3, 4 * C, 4), a("io2"), cfix, ALU.is_ge, w3, ALU.mult)
-        scan(a("EY", 0, 160), a("Mr", 0, 160), a("EX", 0, 160), 0.0, ALU.add, ALU.max)
+        ts(uS, cnt, 0.5, ALU.mult, 160.0, ALU.add)
+        cp(a("ab"), cnt)
+        tt(a("z", 65, 68), w(0, 3), a("cz", 4, 7), ALU.subtract)
+        tt(a("pre"), ind(w(0, 8), a("xl", 0, 3)), a("cst"), ALU.subtract)
+        tt(a("z", 0, 64), ind(a("io2"), uS), a("c64"), ALU.subtract)
+        above(0)
+        above(1)
+        reduce(red, a("z", 0, 64), ALU.min)
+        scan(a("Ms", 0, 68), a("h68"), a("z"), 0.0, ALU.add, ALU.min)
+        rows("A", 3)
+        above(2)
+        above(3)
+        ts(a("Y", 1, 80, 4), a("pre", 0, 40, 2), red, ALU.subtract, -1279.0, ALU.add)
+        tt(a("Y", 0, 96, 2), ind(a("Ms"), a("xl", 4, 7)), a("pre"), ALU.subtract)
         quant("hs", 0, C, a("hs"))
-        mm(1, "one", 0, "hs", 0, C)
-        act(a("X"), ps(1), ACT.Copy)
-        rows("B", rowB, keyB, 12, 16, 256, T3)
-        rows("B", rowB, keyB, 8, 12, 192, T2)
-        e2, e1, e3 = a("EY", 3, 80, 4), a("EY", 83, 160, 4), a("EY", 160, 180)
-        fr, z, zf, pos = (a("sm2", 100 + 20 * j, 120 + 20 * j) for j in range(4))
-        tt(fr, e1, e2, ALU.is_ge)
-        ts(z, e2, c1("Z", 128), ALU.subtract, -1.0, ALU.mult)
-        tt(e3, e1, a("CX", 160, 180), ALU.add)
-        quant("B", QU, QU + 128, a("tB", TU, TU + 512))
-        tt(zf, z, fr, ALU.mult)
-        tt(pos, zf, e3, ALU.max)
-        cols("B", T4, Q4, 256, start=True)
-        mm(BANK["B"], "one", 0, "B", QU + 64, QU + 192, False, False)
-        cp(uP, pos)
-        tt(a("kC"), ind(a("X"), uP), a("krow"), ALU.add)
-        scan(a("eC"), a("M16"), a("kC"), 0.0, ALU.add, ALU.max)
-        ts(a("sm2", 180, 200), a("eC", 15, C, 16), K16, ALU.subtract)
-        cols("B", T3, Q3, 192)
-
-        rowC, keyC = (lambda w: a("kC", 0, w)), (lambda m: c1("sm2", 180 + m))
-        rows("C", rowC, keyC, 16, 20, 320, T4)
-        rows("C", rowC, keyC, 12, 16, 256, T3)
-        rows("C", rowC, keyC, 8, 12, 192, T2)
-        share("C", rowC, keyC, 0, 4)
-        cols("B", T2, Q2, 128, stop=True)
-        share("C", rowC, keyC, 4, 7)
-        extract("B")
-        share("C", rowC, keyC, 7, 8)
-        dB = lead("B")
-        share("C", rowC, keyC, 8, 9)
-        ts(uB, dB, 0.5, ALU.mult, colB, ALU.add)
-        share("C", rowC, keyC, 9, 12)
-        cols("C", T4, Q4, 256, start=True)
-        shared("C", 0)
-        shared("C", 1)
-        shared("C", 2)
-        cols("C", T3, Q3, 192, stop=True)
-        scatter(a("orow"), uB, a("I", 0, C))
-        act(a("mrow"), ind(a("orow"), uP), ACT.Copy)
-        if t == 0:
-            lin(a("M4"), a("nm4"), K + BIG, -BIG)
-        extract("C")
-        dC = lead("C")
-        ts(uC, dC, 0.5, ALU.mult, colB, ALU.add)
-        scatter(a("brow"), uC, a("mrow"))
-        scan(a("eo", C, C + L), a("M4", 0, L), a("brow", 0, L), 0.0, ALU.add, ALU.max)
+        mm(1, "k", ONE, "hs", 0, C)
+        pack("A", 4)
+        cols("A", 4)
+        rows("A", 2)
+        scan(a("Yo"), a("d4"), a("Y", 0, 80), 0.0, ALU.mult, ALU.max)
+        keysB(H, C, 0)
+        pack("A", 3)
+        cols("A", 3)
+        ts(a("sm2", 60, 80), pos2, 640.0, ALU.is_ge, -640.0, ALU.mult)
+        keysB(H, C, 1)
+        scp(a("X", 0, C), ps(1))
+        lin(a("X", C, 2 * C), ps(1), 1.0, -640.0)
+        ts(uQ, pos2, 0.5, ALU.mult)
+        keysB(0, H, 0)
+        pack("A", 2)
+        cols("A", 2, stop=True)
+        keysB(H, C, 2)
+        keysB(0, H, 1)
+        scp(a("Xg", 160, C), ind(a("X"), a("ul", 120, 130)))
+        cp(a("Xg", 0, 160), ind(a("X"), a("ul", 110, 120)))
+        keysB(H, C, 3)
+        keysB(0, H, 2)
+        wrap("ext", a("Xg"), C, 2 * C)
+        rows("B", 1)
+        keysB(0, H, 3)
+        tt(a("sm2", 60, 80), a("sm2", 60, 80), pos2, ALU.add)
+        rows("B", 4)
+        for m in range(20):
+            ts(a("tX", 4 * (5 - m % 5) + m // 5, 4 * C + 4, 20), a("LV", 4 - m % 5 + m, C + m, 5), c1("ext", C + 16 * m + 15), ALU.is_equal)
+        if first:
+            later_constants(3)
+        pack("B", 1)
+        tt(a("dm"), a("ext", C + 15, 2 * C, 16), a("cdm"), ALU.add)
+        quant("X", 0, C, a("tX", 4, 4 * C + 4))
+        mm(1, "k", PRE, "X", 0, C, True, False)
+        rows("B", 3)
+        quant("X", C, 2 * C, a("tX", 0, 4 * C))
+        mm(1, "k", SUF, "X", C, 2 * C, False, True)
+        same(a("es", 5, 20), 1)
+        same(a("es", 20, 30), 2)
+        pack("B", 4)
+        cols("B", 4, start=True)
+        cols("B", 1)
+        tt(a("es", 10, 20), a("es", 10, 20), a("es", 20, 30), ALU.add)
+        rows("B", 2)
+        ts(uD, a("dm"), 0.5, ALU.mult, 160.0, ALU.add)
+        ts(uP, a("sm2", 60, 80), 0.5, ALU.mult)
+        same(a("es", 30, 35), 3)
+        scan(a("G"), ps(1), zeros, 0.0, ALU.add, ALU.add)
+        wrap("ext", ps(4, 64, 128), 192, 256)
+        pack("B", 3)
+        cols("B", 3)
+        scp(a("Gg", 160, C), ind(a("G"), a("ul", 90, 100)))
+        cp(a("Gg", 0, 160), ind(a("G"), a("ul", 80, 90)))
+        tt(a("es", 15, 20), a("es", 15, 20), a("es", 30, 35), ALU.add)
+        scp(a("prow"), ind(a("I"), uQ))
+        pack("B", 2)
+        cols("B", 2, stop=True)
+        wrap("ext", a("Gg"), C, 2 * C)
+        rows("B", 0)
+        positions(192, C, 0)
+        if first:
+            later_constants(4)
+        tt(a("sm2", 40, 60), a("ext", C + 15, 2 * C, 16), a("es", 0, 20), ALU.add)
+        positions(192, C, 1)
+        wrap("ext", ps(6, 0, 192), 0, 192)
+        ts(uC, a("sm2", 40, 60), K16, ALU.subtract)
+        positions(192, C, 2)
+        scp(a("TLg"), ind(a("TL"), uC))
+        positions(0, 192, 0)
+        scatter(a("lp"), uC, a("prow"))
+        if not first:
+            scp(a("TLn"), ind(a("TLg"), a("pm")))
+            unpack(t)
+        positions(0, 192, 1)
+        wrap("eo", a("lp", 0, L), C + L, C + 2 * L)
+        positions(0, 192, 2)
+        ts(uL, a("eo", C + L + 15, C + 2 * L, 16), K16, ALU.subtract)
+        if first:
+            wrap("px", a("pr"), 0, C)
+        scp(a("otj"), ind(a("orow"), uP))
+        cp(a("brow"), ind(a("orow"), uL))
+        if first:
+            ts(a("pm"), a("px", 15, C, 16), K16, ALU.subtract)
+            scp(a("TLn"), ind(a("TLg"), a("pm")))
+        scan(a("eo", C, C + L), a("M4", 0, L), a("brow"), 0.0, ALU.add, ALU.max)
         ts(a("sl%d" % t), a("eo", C + 3, C + L, 4), 4.0, ALU.mult, col4, ALU.add)
         send(t, "l", a("sl%d" % t))
 
-        if t == 0:
+        if first:
             quant("E", 0, 512, a("E"))
-        for b in range(4):
-            mm(4 + b, "E", 128 * b, "L%d" % t, 0, C)
-        for b in range(4):
-            act(a("D", b, 4 * C, 4), ps(4 + b), ACT.Copy)
-        tt(a("otr"), ind(a("TL"), uC), a("mrow"), ALU.max)
-        if t == 0:
+            unpack(t)
+        tt(a("otr"), ind(a("otj"), a("pm")), a("TLn"), ALU.max)
+        if first:
             quant("v", 0, 128, a("vb"))
         scan(a("eo", 0, C), a("M4"), a("otr"), 0.0, ALU.add, ALU.max)
         ts(a("off"), a("eo", 3, C, 4), 4.0, ALU.mult, col4, ALU.add)
         if t == R - 1:
             dma("y", T.ot[:], T.otr[0:128:16, :], [a("otr")], [], "dout")
-
-        ll = "ll%d" % t
-        cp(a(tw, 4 * C, 4 * C + 2 * L), ind(a("D"), a(ll, 0, 12)))
-        act(a(tw, 4 * C + 2 * L, 4 * C + 4 * L), ind(a("D"), a(ll, 12, 24)), ACT.Copy)
-        cp(a("V", 0, 2 * C), ind(a(tw), a("off", 0, 40)))
-        act(a("V", 2 * C, 4 * C), ind(a(tw), a("off", 40, 80)), ACT.Copy)
-        quant("V", 0, C, a("V"))
-        for b in (0, 3, 1, 2):
-            mm(4 + b, "w", 128 * b, "V", 0, C)
-        act(a("V64", 0, 4 * C, 4), a("V", 0, 4 * C, 4), ACT.Copy, None, 64.0)
-        act(a("V64", 2, 4 * C, 4), a("V", 2, 4 * C, 4), ACT.Copy, None, 64.0)
-        ts(a("V64", 1, 4 * C, 4), a("V", 1, 4 * C, 4), 64.0, ALU.mult)
-        act(a("tmp", 3 * C, 4 * C), ps(7), ACT.Copy, None, 0.015625)
-        for b in range(3):
-            tt(a("tmp", b * C, b * C + C), ps(4 + b), a("V64", b, 4 * C, 4), ALU.add)
-            act(a(nx, b, 4 * C, 4), a("tmp", b * C, b * C + C), ACT.Copy, None, 0.015625)
-        tt(a(nx, 3, 4 * C, 4), a("tmp", 3 * C, 4 * C), a("V", 3, 4 * C, 4), ALU.add)
+        new_state(t)
 
     last = "T%d" % R
-    quant(last, 0, 160, a("tw%d" % R, 0, 640))
-    quant(last, 160, C, a("tw%d" % R, 640, 4 * C))
-    mm(0, "v", 0, last, 0, 160)
-    mm(1, "v", 0, last, 160, C)
-    cp(a("yb", 0, 160), ps(0, 160))
-    act(a("yb", 160, C), ps(1, 160), ACT.Copy)
+    mm(4, "v", 0, last, 0, H)
+    quant(last, H, C, a("tw%d" % R, 4 * H, 4 * C))
+    mm(5, "v", 0, last, H, C)
+    scp(a("yb", 0, H), ps(4, 0, H))
+    cp(a("yb", H, C), ps(5, 0, C - H))
     dma("y", T.oc[:], T["q" + last][:].bitcast(dt.uint8), [a("q" + last)], [], "dout")
     for k in range(4):
         dma("y", T.osc[4 * k:4 * k + 4, :], T["s" + last][32 * k:32 * k + 4, :], [a("s" + last)], [], "dout")

@@ -7,6 +7,7 @@ H = 192
 STEP = [1, 2, 4]
 K = 262144.0
 BIG = 32 * K
+KEY0 = 2 ** 21 + 320 * (319 + 320)
 F32, BF, I32, U16, X4, U8 = "float32", "bfloat16", "int32", "uint16", "float8_e4m3fn_x4", "uint8"
 TILE = {4: (0, 0), 3: (1280, 256), 2: (2304, 448)}
 ONE, W320, PRE, SUF = 0, 128, 256, 384
@@ -40,24 +41,23 @@ for _t in range(R):
     _pair("R%d" % _t, C)
     for _n in ("ll", "rl", "sl"):
         _sb("%s%d" % (_n, _t), 24, U16)
-for _n, _w in (("u", 128), ("S", 128), ("v", 128), ("w", 512), ("k", 512), ("E", 512), ("bits", C), ("hs", C),
-               ("V", C), ("A", 576), ("B", 576), ("U", 256), ("X", 2 * C)):
+for _n, _w in (("u", 128), ("S", 128), ("v", 128), ("w", 512), ("k", 512), ("E", 512), ("bits", C),
+               ("V", C), ("A", 832), ("B", 576), ("U", 256), ("X", 2 * C)):
     _pair(_n, _w)
-for _n, _w in (("ub", 512), ("vb", 512), ("kc", 2048), ("E", 2048), ("bits", 4 * C), ("hs", 4 * C), ("tA", 3072),
+for _n, _w in (("ub", 512), ("vb", 512), ("kc", 2048), ("E", 2048), ("bits", 4 * C), ("hs", 4 * C), ("tA", 4096),
                ("tB", 3072), ("tU", 768), ("t0", 256), ("tX", 4 * C + 16), ("io2", C + 32),
                ("D", 4 * C), ("V", 4 * C), ("V64", 4 * C), ("tmp", 4 * C)):
     _sb(_n, _w, BF)
-for _n, _w in (("I", 2 * C), ("J", 640), ("TL", C), ("W", C + 8), ("Ms", 72), ("X", 2 * C), ("G", C), ("lp", C),
+for _n, _w in (("I", C + H), ("J", 640), ("TL", C), ("W", C + 8), ("Ms", 72), ("G", C), ("lp", C),
                ("orow", C), ("otj", C), ("TLg", C), ("otr", C), ("yb", C)):
     _sb(_n, _w, F32)
-_parts("kb", BF, (("j16", C), ("g8", 512), ("j4", C), ("cb", 4), ("mask", C), ("nmask", C), ("nm4", C),
+_parts("kb", BF, (("j16", C), ("g8", 512), ("cb", 4), ("mask", C), ("nmask", C), ("nm4", C),
                   ("M16", C), ("M8", C), ("M4", C), ("h68", 68), ("d4", 80), ("neg", 16)))
-_parts("kf", F32, (("cf", 4), ("col", 16), ("pw", 24), ("p8", 16), ("crow", C), ("cst", 48), ("cdm", 20), ("cz", 8),
-                   ("c64", 64), ("LV", C + 32), ("pr", C), ("px", C)))
-_parts("db", BF, (("ab", 4),))
+_parts("kf", F32, (("cf", 4), ("col", 16), ("pw", 24), ("p8", 16), ("cst", 48), ("cdm", 20), ("cz", 8),
+                   ("c64", 64), ("LV", 68), ("pr", C), ("px", C)))
 _parts("df", F32, (("sm", C), ("sx", C), ("hk", C), ("acc", 48), ("ext", 2 * C), ("z", 68), ("pre", 48), ("Y", 96),
-                   ("Yo", 80), ("dm", 20), ("TLn", C), ("sm2", 80), ("Xg", C), ("kB", C), ("kx", C), ("Gg", C),
-                   ("prow", C), ("es", 40), ("brow", L), ("eo", C + 2 * L)))
+                   ("Yo", 80), ("dm", 20), ("TLn", C), ("sm2", 100), ("kB", C), ("kx", C), ("Gg", C),
+                   ("prow", C), ("es", 40), ("Sg", 64), ("h2", 20), ("brow", L), ("eo", C + 2 * L)))
 for _n, _w in (("ip", 16), ("q5", 24)):
     _sb(_n, _w, I32)
 for _n, _w in (("pk", 8), ("xl", 8), ("pm", 20), ("ul", 132), ("off", 80)):
@@ -269,88 +269,90 @@ def rank_program(g, core, T, topo):
     K16, c4a, col4, colB, powc, thr0, cz0, c40, c40k, cLV, cy, off16, q103, odd4 = (c1("col", j) for j in range(14))
     f8 = c1("p8", 15)
     iota(a("ip", 0, 1), [[0, 1]], 0, 1)
-    iota(a("j16"), [[0, 20], [1, 16]])
     iota(a("ip", 8, 16), [[16, 8]], 8, 0)
-    iota(a("I", 0, C), [[1, C]])
+    iota(a("j16"), [[0, 20], [1, 16]])
+    iota(a("I", 0, 68), [[1, 68]])
     iota(a("g8"), [[1, 8], [0, 64]])
     iota(a("q5", 0, 3), [[16 * 103, 3]])
     iota(a("io2"), [[2, C + 32]], -320)
     iota(a("c64"), [[10, 4], [40, 16]], -310)
+    iota(a("I", 68, C), [[1, C - 68]], 68)
+    iota(a("J"), [[-320, 640]], KEY0)
+    iota(a("hk", 128, 256), [[1, 128]], KEY0 - 320 * (320 + 127))
     fill(a("pw", 0, 6), 2.0)
-    fill(a("d4"), 0.0)
-    fill(a("h68", 64, 68), 0.0)
-    fill(a("neg"), -1.0)
+    fill(a("bits"), 0.0)
     ts(c1("ip", 4), c1("ip", 0), 15, ALU.bitwise_and)
     ts(c1("ip", 5), c1("ip", 0), 4, ALU.logical_shift_right)
     ts(c1("ip", 6), c1("ip", 0), 3, ALU.bitwise_and)
     ts(c1("ip", 7), c1("ip", 0), 12, ALU.bitwise_and)
     ts(c1("q5", 20), c1("ip", 0), 1, ALU.bitwise_and)
     scan(a("pw", 8, 14), a("pw", 0, 6), a("pw", 0, 6), 320.0, ALU.mult, ALU.max)
-    fill(a("d4", 1, 80, 4), -4096.0)
-    fill(a("d4", 2, 80, 4), -1.0)
-    cp(a("cf"), a("ip", 4, 8))
+    cp(a("pk"), a("ip", 8, 16))
     cp(a("cb"), a("ip", 4, 8))
-    fill(a("bits"), 0.0)
+    cp(a("cf"), a("ip", 4, 8))
+    quant("U", 128, 256, a("bits", 0, 512))
+    ts(odd4, c1("q5", 20), 4.0, ALU.mult)
     ts(a("mask"), a("j16"), b0, ALU.is_equal)
     ts(a("nmask"), a("j16"), b0, ALU.not_equal)
-    cp(a("pk"), a("ip", 8, 16))
-    fill(a("tU", 0, 256), 0.0)
-    tt(a("pw", 16, 22), a("pw", 8, 14), a("mask", 0, 6), ALU.mult)
-    ts(a("M8"), a("nmask"), 8.0, ALU.mult)
     ts(a("h68", 0, 64), a("j16", 0, 64), b0, ALU.is_ge, -1024.0, ALU.mult)
-    quant("U", 128, 256, a("bits", 0, 512))
-    reduce(powc, a("pw", 16, 22), ALU.add)
-    for x in (a("W", C, C + 8), a("Ms"), a("Y"), a("z", 64, 68), a("tX", 0, 16), a("es", 0, 5)):
-        fill(x, 0.0)
-    ts(odd4, c1("q5", 20), 4.0, ALU.mult)
-    scan(a("p8"), a("M8", 0, 16), a("neg"), 0.0, ALU.mult, ALU.min)
-    ts(a("kc", 512, 1024), a("g8"), bg, ALU.is_equal, 320.0, ALU.mult)
+    tt(a("pw", 16, 22), a("pw", 8, 14), a("mask", 0, 6), ALU.mult)
+    for x, width, value in ((a("d4"), 80, 0.0), (a("h68", 64, 68), 4, 0.0), (a("W", C, C + 8), 8, 0.0), (a("Ms"), 72, 0.0),
+                            (a("z", 64, 68), 4, 0.0), (a("Y"), 96, 0.0), (a("tX", 0, 16), 16, 0.0), (a("es", 0, 5), 5, 0.0),
+                            (a("tU", 0, 256), 256, 0.0), (a("neg"), 16, -1.0), (a("d4", 1, 80, 4), 20, -4096.0),
+                            (a("d4", 2, 80, 4), 20, -1.0)):
+        lin(x, a("bits", 1, 4 * width, 4), 1.0, value)
     for col, scale, bias in ((q103, 103.0, 0.0), (off16, -1024.0, 16384.0), (thr0, 4 * 204800.0, 102400.0), (K16, -K, 15 * K),
-                             (cz0, 40.0, -310.0), (c40, 40.0, -319.0), (cy, 40.0, 0.0), (c40k, K - 40.0, 318.0 - 15 * K),
-                             (cLV, 40.0 - K, 15 * K - 318.0), (colB, -K / 2, 7.5 * K + 159.5)):
+                             (cz0, 40.0, -310.0)):
+        lin(col, c0, scale, bias)
+    quant("u", 0, 128, a("ub"))
+    reduce(powc, a("pw", 16, 22), ALU.add)
+    pick = a("pk")
+    op("s", [a("su"), pick], [a("sS")], lambda: g.scalar.activation(T.sS[:], T.su[:].indirect(pick[0]), ACT.Copy))
+    op("v", [a("qu"), pick], [a("qS")], lambda: g.vector.tensor_copy(T.qS[:].bitcast(dt.uint32), T.qu[:].bitcast(dt.uint32).indirect(pick[0])))
+    quant("T0", 0, H, a("tw0", 0, 4 * H))
+    ts(a("kc", 512, 1024), a("g8"), bg, ALU.is_equal, 320.0, ALU.mult)
+    for col, scale, bias in ((c40, 40.0, -319.0), (cy, 40.0, 0.0), (c40k, -40.0, 638.0), (cLV, 8.0, -190.0),
+                             (colB, -K / 2, 7.5 * K + 159.5)):
         lin(col, c0, scale, bias)
     lin(c4a, c3, K, c2)
-    lin(a("M16"), a("nmask"), K + BIG, -BIG)
-    lin(col4, c4a, 1.0, -12 * K)
     lin(a("cz", 0, 4), a("I", 0, 4), 204800.0, thr0)
     lin(a("cz", 4, 8), a("I", 0, 4), 10.0, cz0)
     lin(a("cst", 0, 48, 2), a("I", 0, 24), 2.0, c40)
     lin(a("cst", 1, 48, 2), a("I", 0, 24), 2.0, cy)
     lin(a("cdm"), a("I", 0, 20), -2.0, c40k)
     lin(a("ext", 256 + 15, C, 16), a("I", 0, 4), 0.0, K16)
-    lin(a("crow"), a("I", 0, C), 1.0, 2301632.0)
-    lin(a("J", 0, C), a("I", 0, C), -320.0, 0.0)
-    quant("u", 0, 128, a("ub"))
-    ts(a("h68", 16, 68, 16), a("h68", 16, 68, 16), off16, ALU.add)
-    quant("k", W320, W320 + 128, a("kc", 512, 1024))
-    ts(a("q5", 8, 11), a("q5", 0, 3), q103, ALU.add)
-    pick = a("pk")
-    op("v", [a("qu"), pick], [a("qS")], lambda: g.vector.tensor_copy(T.qS[:].bitcast(dt.uint32), T.qu[:].bitcast(dt.uint32).indirect(pick[0])))
-    op("s", [a("su"), pick], [a("sS")], lambda: g.scalar.activation(T.sS[:], T.su[:].indirect(pick[0]), ACT.Copy))
+    lin(a("LV"), a("I", 0, 68), 2.0, cLV)
+    lin(col4, c4a, 1.0, -12 * K)
     lin(a("kc", 0, 512), a("kc", 512, 1024), 1.0 / 320, 0.0)
-    lin(a("J", C, 2 * C), a("I", 0, C), -320.0, -102400.0)
-    lin(a("LV"), a("io2"), 1.0, cLV)
-    scp(a("I", C, 2 * C), a("I", 0, C))
-    lin(a("TL", 0, L), a("I", 0, L), 1.0, 320.0)
-    lin(a("TL", L, C), a("I", L, C), 0.0, 0.0)
-    ts(a("q5", 16, 19), a("q5", 8, 11), 10, ALU.logical_shift_right)
+    scp(a("M8"), a("nmask"), 8.0)
+    lin(a("M16"), a("nmask"), K + BIG, -BIG)
     select(a("kc", 1024, 1536), a("kc", 0, 512), [[1, 128], [0, 4]], ALU.is_gt, 0, -1)
     select(a("kc", 1536, 2048), a("kc", 0, 512), [[-1, 128], [0, 4]], ALU.is_ge, 0, 1)
 
     def later_constants(step):
-        if step == 1:
-            ts(a("xl", 4, 7), a("q5", 16, 19), 3.0, ALU.min, 64.0, ALU.add)
-            ts(a("xl", 0, 3), a("q5", 16, 19), 3.0, ALU.min, odd4, ALU.max)
-            quant("k", ONE, ONE + 128, a("kc", 0, 512))
-        if step == 2:
+        if step == 0:
+            quant("k", W320, W320 + 128, a("kc", 512, 1024))
+            ts(a("q5", 8, 11), a("q5", 0, 3), q103, ALU.add)
+            ts(a("h68", 16, 68, 16), a("h68", 16, 68, 16), off16, ALU.add)
+            iota(a("I", C, C + H), [[1, H]])
+            iota(a("TL", 0, L), [[1, L]], 320)
+            iota(a("TL", L, C), [[0, C - L]])
+            iota(a("pr"), [[1, 16], [16, 20]])
             for b in range(4):
                 select(a("E", 512 * b, 512 * b + 512), a("kc", 0, 512), [[-1, 512]], ALU.is_equal, b, 4)
-            iota(a("j4"), [[0, 80], [4, 4]])
-            iota(a("pr"), [[1, 16], [16, 20]])
+        if step == 1:
+            ts(a("q5", 16, 19), a("q5", 8, 11), 10, ALU.logical_shift_right)
+            scan(a("p8"), a("M8", 0, 16), a("neg"), 0.0, ALU.mult, ALU.min)
+        if step == 2:
+            ts(a("xl", 4, 7), a("q5", 16, 19), 3.0, ALU.min, 64.0, ALU.add)
+            ts(a("xl", 0, 3), a("q5", 16, 19), 3.0, ALU.min, odd4, ALU.max)
         if step == 3:
             quant("k", PRE, PRE + 256, a("kc", 1024, 2048))
-        if step == 4:
-            ts(a("nm4"), a("j4"), b3, ALU.not_equal)
+            quant("k", ONE, ONE + 128, a("kc", 0, 512))
+        if step >= 4:
+            for j in (2 * step - 8, 2 * step - 7):
+                ts(a("nm4", 80 * j, 80 * j + 80), a("j16", 0, C, 4), b3, ALU.not_equal)
+        if step == 5:
             lin(a("M4"), a("nm4"), K + BIG, -BIG)
 
     ACC = {"A": 0, "B": 24}
@@ -373,12 +375,17 @@ def rank_program(g, core, T, topo):
                 act(o, a("kB", 0, w), ACT.Sign, c1("kx", 16 * m + 15), f8, c1("acc", ACC[x] + m))
 
     def pack(x, k):
-        if k == 1:
+        if x == "A" and k < 2:
+            quant("A", 576 + 128 * k, 704 + 128 * k, a("tA", 3072 + 512 * k, 3584 + 512 * k))
+        elif k == 1:
             quant("U", 0, 128, a("tU", 0, 512))
         else:
             quant(x, TILE[k][1], TILE[k][1] + 64 * k, a("t" + x, TILE[k][0], TILE[k][0] + 256 * k))
 
     def cols(x, k, start=False, stop=False):
+        if x == "A" and k < 2:
+            mm(BANK[x], "k", STAT[x], x, 576 + 128 * k, 704 + 128 * k, start, stop)
+            return
         if k == 1:
             mm(BANK[x], "k", STAT[x], "U", 64, 192, start, stop)
             return
@@ -401,7 +408,7 @@ def rank_program(g, core, T, topo):
         if step == 0:
             ts(u, a("acc", lo // 16, hi // 16), 320.0, ALU.add)
         elif step == 1:
-            tt(part, ind(a("J"), u), a("crow", lo, hi), ALU.add)
+            tt(part, ind(a("J"), u), a("I", lo, hi), ALU.add)
         elif step == 2:
             tt(row, ps(4, lo - 128, hi - 128) if lo else ps(3, lo, hi), part, ALU.add)
         else:
@@ -419,8 +426,13 @@ def rank_program(g, core, T, topo):
     def w(lo, hi=None):
         return a("W", C + lo, C + (lo + 1 if hi is None else hi))
 
-    def above(j):
-        ts(a("hs", j, 4 * C, 4), a("io2", 0, C), c1("ab", j), ALU.is_ge, 10.0, ALU.mult)
+    def share(m0, m1):
+        for m in range(m0, m1):
+            ts(a("tA", 3072 + 512 * (m // 4) + m % 4, 3584 + 512 * (m // 4), 4), ps(6, 0, 128), c1("sx", 16 * m + 15), ALU.is_lt, 2.0, ALU.mult)
+
+    def levels(m0, m1):
+        for m in range(m0, m1):
+            ts(a("tX", 4 * (5 - m % 5) + m // 5, 4 * C + 4, 20), a("LV", m // 5, m // 5 + 64), c1("sm2", 60 + m), ALU.add, c1("h2", m), ALU.is_equal)
 
     def same(out, k):
         tt(out, a("dm", 5 * k, 20), a("dm", 0, 20 - 5 * k), ALU.is_equal)
@@ -473,11 +485,10 @@ def rank_program(g, core, T, topo):
         quant("T%d" % (t + 1), 0, H, a(nx, 0, 4 * H))
         down(H, C, 3)
 
-    uC, uP, uD, uL, uS, uQ = (a("ul", lo, hi) for lo, hi in ((40, 60), (60, 80), (80, 100), (100, 106), (106, 110), (110, 130)))
+    uC, uP, uD, uL, uS = (a("ul", lo, hi) for lo, hi in ((40, 60), (60, 80), (80, 100), (100, 106), (106, 110)))
     zeros = a("bits", 1, 4 * C, 4)
-    cnt, red, pos2 = w(0, 4), c1("es", 36), a("Yo", 2, 80, 4)
+    cnt, red, pos2, free = w(0, 4), c1("es", 36), a("Yo", 2, 80, 4), a("sm2", 60, 80)
 
-    quant("T0", 0, H, a("tw0", 0, 4 * H))
     for t in range(R):
         tw, qT = "tw%d" % t, "T%d" % t
         first = t == 0
@@ -485,131 +496,131 @@ def rank_program(g, core, T, topo):
         mm(6, "S", 0, qT, 0, H)
         mm(7, "u", 0, qT, 0, H)
         mm(5, "S", 0, qT, 0, H)
-        if first:
-            later_constants(1)
         quant(qT, H, C, a(tw, 4 * H, 4 * C))
         mm(1, "u", 0, qT, H, C)
         mm(4, "S", 0, qT, H, C)
         send(t, "q", a("q" + qT))
         send(t, "s", a("s" + qT))
         if first:
-            later_constants(2)
+            later_constants(0)
         keysA(6, 0, H, 0)
         bits(7, 0, H)
         keysA(6, 0, H, 1)
         bits(1, H, C)
         quant("bits", 0, H, a("bits", 0, 4 * H))
-        rows("A", 0)
-        rows("A", 1)
+        rows("A", 2)
         quant("bits", H, C, a("bits", 4 * H, 4 * C))
-        keysA(4, H, C, 0)
+        mm(3, "k", W320, "bits", 0, 192, True, False)
         mm(2, "k", W320, "bits", 0, C)
         mm(7, "k", W320, "bits", 0, C)
         mm(0, "S", 0, qT, 0, C)
-        mm(3, "k", W320, "bits", 0, 192, True, False)
-        keysA(4, H, C, 1)
+        share(4, 8)
+        keysA(4, H, C, 0)
+        if first:
+            later_constants(1)
+
         for j in range(1, 4):
             act(a("tB", j, 4 * C, 4), ps(2), ACT.Sign, c1("cz", j), -1.0, w(j))
         ts(a("tB", 0, 4 * C, 4), ps(7), c1("cz", 0), ALU.is_le, 2.0, ALU.mult)
-        pack("A", 1)
-        cols("A", 1)
+        keysA(4, H, C, 1)
         mm(4, "k", W320, "bits", 128, C, True, False)
+        if first:
+            later_constants(2)
         scan(a("W", 1, C + 1), a("tB", 0, 4 * C, 4), zeros, -320.0, ALU.add, ALU.add)
         rows("A", 4)
+        pack("A", 1)
+        keysB(128, H, 0)
 
         ts(uS, cnt, 0.5, ALU.mult, 160.0, ALU.add)
-        cp(a("ab"), cnt)
+        share(2, 4)
         tt(a("z", 65, 68), w(0, 3), a("cz", 4, 7), ALU.subtract)
-        tt(a("pre"), ind(w(0, 8), a("xl", 0, 3)), a("cst"), ALU.subtract)
         tt(a("z", 0, 64), ind(a("io2"), uS), a("c64"), ALU.subtract)
-        above(0)
-        above(1)
-        reduce(red, a("z", 0, 64), ALU.min)
-        scan(a("Ms", 0, 68), a("h68"), a("z"), 0.0, ALU.add, ALU.min)
+        share(0, 2)
+        tt(a("pre"), ind(w(0, 8), a("xl", 0, 3)), a("cst"), ALU.subtract)
         rows("A", 3)
-        above(2)
-        above(3)
-        ts(a("Y", 1, 80, 4), a("pre", 0, 40, 2), red, ALU.subtract, -1279.0, ALU.add)
+        lin(a("Sg"), ind(a("io2"), uS), 1.0, 319.0)
+        scan(a("Ms", 0, 68), a("h68"), a("z"), 0.0, ALU.add, ALU.min)
+        reduce(red, a("z", 0, 64), ALU.min)
+        pack("A", 2)
+        pack("A", 0)
         tt(a("Y", 0, 96, 2), ind(a("Ms"), a("xl", 4, 7)), a("pre"), ALU.subtract)
-        quant("hs", 0, C, a("hs"))
-        mm(1, "k", ONE, "hs", 0, C)
-        pack("A", 4)
-        cols("A", 4)
-        rows("A", 2)
+        ts(a("Y", 1, 80, 4), a("pre", 0, 40, 2), red, ALU.subtract, -639.0, ALU.add)
+        keysB(128, H, 1)
         scan(a("Yo"), a("d4"), a("Y", 0, 80), 0.0, ALU.mult, ALU.max)
+        pack("A", 4)
+        for k in (0, 1, 2, 4):
+            cols("A", k)
+
+        for m in range(20):
+            act(a("hs", 64 * m, 64 * m + 64), a("Sg"), ACT.Sign, c1("Yo", 4 * m + 2), -1.0, c1("h2", m))
+        ts(free, a("Yo", 0, 80, 4), 0.0, ALU.is_gt, 128.0, ALU.mult)
         keysB(H, C, 0)
         pack("A", 3)
-        cols("A", 3)
-        ts(a("sm2", 60, 80), pos2, 640.0, ALU.is_ge, -640.0, ALU.mult)
+        cols("A", 3, stop=True)
         keysB(H, C, 1)
-        scp(a("X", 0, C), ps(1))
-        lin(a("X", C, 2 * C), ps(1), 1.0, -640.0)
-        ts(uQ, pos2, 0.5, ALU.mult)
-        keysB(0, H, 0)
-        pack("A", 2)
-        cols("A", 2, stop=True)
+        levels(0, 5)
         keysB(H, C, 2)
-        keysB(0, H, 1)
-        scp(a("Xg", 160, C), ind(a("X"), a("ul", 120, 130)))
-        cp(a("Xg", 0, 160), ind(a("X"), a("ul", 110, 120)))
-        keysB(H, C, 3)
         keysB(0, H, 2)
-        wrap("ext", a("Xg"), C, 2 * C)
-        rows("B", 1)
+        levels(5, 10)
         keysB(0, H, 3)
-        tt(a("sm2", 60, 80), a("sm2", 60, 80), pos2, ALU.add)
         rows("B", 4)
-        for m in range(20):
-            ts(a("tX", 4 * (5 - m % 5) + m // 5, 4 * C + 4, 20), a("LV", 4 - m % 5 + m, C + m, 5), c1("ext", C + 16 * m + 15), ALU.is_equal)
+        levels(10, 20)
+        tt(a("sm2", 20, 40), a("h2"), free, ALU.subtract)
+        ts(uP, pos2, 0.5, ALU.mult)
         if first:
             later_constants(3)
-        pack("B", 1)
-        tt(a("dm"), a("ext", C + 15, 2 * C, 16), a("cdm"), ALU.add)
+
         quant("X", 0, C, a("tX", 4, 4 * C + 4))
         mm(1, "k", PRE, "X", 0, C, True, False)
-        rows("B", 3)
+        ts(a("sm2", 80, 100), a("sm2", 20, 40), 5.0, ALU.mult)
         quant("X", C, 2 * C, a("tX", 0, 4 * C))
         mm(1, "k", SUF, "X", C, 2 * C, False, True)
-        same(a("es", 5, 20), 1)
-        same(a("es", 20, 30), 2)
+        rows("B", 3)
+        tt(a("dm"), a("sm2", 80, 100), a("cdm"), ALU.add)
+        keysB(H, C, 3)
         pack("B", 4)
         cols("B", 4, start=True)
-        cols("B", 1)
-        tt(a("es", 10, 20), a("es", 10, 20), a("es", 20, 30), ALU.add)
-        rows("B", 2)
+        same(a("es", 20, 30), 2)
         ts(uD, a("dm"), 0.5, ALU.mult, 160.0, ALU.add)
-        ts(uP, a("sm2", 60, 80), 0.5, ALU.mult)
-        same(a("es", 30, 35), 3)
+        same(a("es", 5, 20), 1)
         scan(a("G"), ps(1), zeros, 0.0, ALU.add, ALU.add)
+        tt(a("es", 10, 20), a("es", 10, 20), a("es", 20, 30), ALU.add)
+        rows("B", 1)
+        rows("B", 2)
+        same(a("es", 30, 35), 3)
         wrap("ext", ps(4, 64, 128), 192, 256)
-        pack("B", 3)
-        cols("B", 3)
-        scp(a("Gg", 160, C), ind(a("G"), a("ul", 90, 100)))
-        cp(a("Gg", 0, 160), ind(a("G"), a("ul", 80, 90)))
+        cp(a("Gg"), ind(a("G"), uD))
         tt(a("es", 15, 20), a("es", 15, 20), a("es", 30, 35), ALU.add)
-        scp(a("prow"), ind(a("I"), uQ))
-        pack("B", 2)
-        cols("B", 2, stop=True)
-        wrap("ext", a("Gg"), C, 2 * C)
-        rows("B", 0)
         positions(192, C, 0)
-        if first:
-            later_constants(4)
-        tt(a("sm2", 40, 60), a("ext", C + 15, 2 * C, 16), a("es", 0, 20), ALU.add)
+        pack("B", 3)
+        wrap("ext", a("Gg"), C, 2 * C)
         positions(192, C, 1)
-        wrap("ext", ps(6, 0, 192), 0, 192)
-        ts(uC, a("sm2", 40, 60), K16, ALU.subtract)
+        pack("B", 1)
+        scp(a("prow"), ind(a("I", 0, C), uP))
+        rows("B", 0)
+        tt(a("sm2", 40, 60), a("ext", C + 15, 2 * C, 16), a("es", 0, 20), ALU.add)
+        pack("B", 2)
+        cols("B", 1)
+        cols("B", 3)
+        cols("B", 2, stop=True)
         positions(192, C, 2)
+        ts(uC, a("sm2", 40, 60), K16, ALU.subtract)
+        wrap("ext", ps(6, 0, 192), 0, 192)
+
         scp(a("TLg"), ind(a("TL"), uC))
-        positions(0, 192, 0)
         scatter(a("lp"), uC, a("prow"))
+        positions(0, 192, 0)
         if not first:
             scp(a("TLn"), ind(a("TLg"), a("pm")))
             unpack(t)
-        positions(0, 192, 1)
+        if first:
+            later_constants(4)
         wrap("eo", a("lp", 0, L), C + L, C + 2 * L)
-        positions(0, 192, 2)
+        positions(0, 192, 1)
+        if first:
+            later_constants(5)
         ts(uL, a("eo", C + L + 15, C + 2 * L, 16), K16, ALU.subtract)
+        positions(0, 192, 2)
         if first:
             wrap("px", a("pr"), 0, C)
         scp(a("otj"), ind(a("orow"), uP))
@@ -635,13 +646,15 @@ def rank_program(g, core, T, topo):
 
     last = "T%d" % R
     mm(4, "v", 0, last, 0, H)
+    dma("y", T.oc[:, 0:4 * H], T["q" + last][:, 0:H].bitcast(dt.uint8), [a("q" + last, 0, H)], [], "dout")
     quant(last, H, C, a("tw%d" % R, 4 * H, 4 * C))
     mm(5, "v", 0, last, H, C)
     scp(a("yb", 0, H), ps(4, 0, H))
     cp(a("yb", H, C), ps(5, 0, C - H))
-    dma("y", T.oc[:], T["q" + last][:].bitcast(dt.uint8), [a("q" + last)], [], "dout")
+    dma("s", T.y[:, 0:H], a("yb", 0, H)[0], [a("yb", 0, H)], [], "dout")
+    dma("y", T.oc[:, 4 * H:4 * C], T["q" + last][:, H:C].bitcast(dt.uint8), [a("q" + last, H, C)], [], "dout")
     for k in range(4):
-        dma("y", T.osc[4 * k:4 * k + 4, :], T["s" + last][32 * k:32 * k + 4, :], [a("s" + last)], [], "dout")
-    dma("s", T.y[:], T.yb[:], [a("yb")], [], "dout")
+        dma("ys"[k % 2], T.osc[4 * k:4 * k + 4, :], T["s" + last][32 * k:32 * k + 4, :], [a("s" + last)], [], "dout")
+    dma("y", T.y[:, H:C], a("yb", H, C)[0], [a("yb", H, C)], [], "dout")
     for sem in count:
         g.wait_ge(T.sem[sem], count[sem])

from concourse.mybir import dt, AluOpType, AxisListType, ActivationFunctionType

ALU = AluOpType
ACT = ActivationFunctionType
C, L, R = 320, 96, 3
H = 192
STEP = [1, 2, 4]
K = 262144.0
BIG = 32 * K
KEY0 = 2 ** 21 + 320 * (319 + 320)
F32, BF, I32, U16, X4, U8 = "float32", "bfloat16", "int32", "uint16", "float8_e4m3fn_x4", "uint8"
TILE = {4: (0, 0), 3: (1280, 256), 2: (2304, 448)}
ONE, W320, PRE, SUF = 0, 128, 256, 384

SCRATCH = {}
PART = {}


def _sb(name, n, d):
    SCRATCH[name] = ("sbuf", [128, n], d)


def _pair(name, n):
    _sb("q" + name, n, X4)
    _sb("s" + name, n, U8)


def _parts(name, d, parts):
    n = 0
    for part, w in parts:
        PART[part] = (name, n, w)
        n += (w + 15) // 16 * 16
    _sb(name, n, d)


for _t in range(R + 1):
    _sb("tw%d" % _t, 4 * C + 4 * L, BF)
    _pair("T%d" % _t, C)
for _t in range(R):
    _pair("L%d" % _t, C)
    _pair("R%d" % _t, C)
    for _n in ("ll", "rl", "sl"):
        _sb("%s%d" % (_n, _t), 24, U16)
for _n, _w in (("u", 128), ("S", 128), ("v", 128), ("w", 512), ("k", 512), ("E", 512), ("bits", C),
               ("V", C), ("A", 832), ("B", 576), ("U", 256), ("X", 2 * C)):
    _pair(_n, _w)
for _n, _w in (("ub", 512), ("vb", 512), ("kc", 2048), ("E", 2048), ("bits", 4 * C), ("hs", 4 * C), ("tA", 4096),
               ("tB", 3072), ("tU", 768), ("t0", 256), ("tX", 4 * C + 16), ("io2", C + 32),
               ("D", 4 * C), ("V", 4 * C), ("V64", 4 * C), ("tmp", 4 * C)):
    _sb(_n, _w, BF)
for _n, _w in (("I", C + H), ("J", 640), ("TL", C), ("W", C + 8), ("Ms", 72), ("G", C), ("lp", C),
               ("orow", C), ("otj", C), ("TLg", C), ("otr", C), ("yb", C)):
    _sb(_n, _w, F32)
_parts("kb", BF, (("j16", C), ("g8", 512), ("cb", 4), ("mask", C), ("nmask", C), ("nm4", C),
                  ("M16", C), ("M8", C), ("M4", C), ("h68", 68), ("d4", 80), ("neg", 16)))
_parts("kf", F32, (("cf", 4), ("col", 16), ("pw", 24), ("p8", 16), ("cst", 48), ("cdm", 20), ("cz", 8),
                   ("c64", 64), ("LV", 68), ("pr", C), ("px", C)))
_parts("df", F32, (("sm", C), ("sx", C), ("hk", C), ("acc", 48), ("ext", 2 * C), ("z", 68), ("pre", 48), ("Y", 96),
                   ("Yo", 80), ("dm", 20), ("TLn", C), ("sm2", 100), ("kB", C), ("kx", C), ("Gg", C),
                   ("prow", C), ("es", 40), ("Sg", 64), ("h2", 20), ("brow", L), ("eo", C + 2 * L)))
for _n, _w in (("ip", 16), ("q5", 24)):
    _sb(_n, _w, I32)
for _n, _w in (("pk", 8), ("xl", 8), ("pm", 20), ("ul", 132), ("off", 80)):
    _sb(_n, _w, U16)
for _b in range(8):
    SCRATCH["ps%d" % _b] = ("psum", [128, 512], F32)

SEMAPHORES = ["ev", "es", "et", "eg", "dx", "dx2", "du", "dw", "dv", "dout", "sent"] + \
    ["%s%d" % (_n, _t) for _n in ("aq", "al") for _t in range(R)]


def _engines(m):
    return bin(m).count("1")


def _route(src, dst, topo):
    if topo.may_write(src, dst):
        return [src, dst]
    able = [c for c in topo.cores_of(src) if c != src and topo.may_write(c, dst)]
    near = [c for c in able if topo.die(c) == topo.die(src)]
    return [src, (near or able)[0], dst]


def _hop(g, T, topo, src, dst, out, in_, sem):
    rid, pid = topo.addr(dst, src)
    m = topo.mask(src, dst)
    g.remote_dma(out, in_, T.sem[sem], T.sem.sent, pid, rid, m)
    return _engines(m)


def _relay(g, core, T, topo):
    n = len(T.cores)
    sent = 0
    for t in range(R):
        for r in range(n):
            way = _route(T.cores[r], T.cores[(r + STEP[t]) % n], topo)
            if len(way) == 3 and way[1] == core:
                e = _engines(topo.mask(way[0], core))
                g.wait_ge(T.sem["aq%d" % t], 2 * e)
                sent += _hop(g, T, topo, core, way[2], T["qL%d" % t][:].bitcast(dt.uint8), T["qR%d" % t][:].bitcast(dt.uint8), "aq%d" % t)
                sent += _hop(g, T, topo, core, way[2], T["sL%d" % t][:], T["sR%d" % t][:], "aq%d" % t)
                g.wait_ge(T.sem["al%d" % t], e)
                sent += _hop(g, T, topo, core, way[2], T["ll%d" % t][:], T["rl%d" % t][:], "al%d" % t)
    if sent:
        g.wait_ge(T.sem.sent, sent)


def rank_program(g, core, T, topo):
    rank = T.rank_of(core)
    if rank is None:
        _relay(g, core, T, topo)
        return
    n = len(T.cores)
    Q = {"v": g.vector, "s": g.scalar, "t": g.tensor, "g": g, "y": g.sync}
    SEM = {"v": "ev", "s": "es", "t": "et", "g": "eg"}
    count = {}
    clock = {e: {} for e in Q}
    log = {}

    def a(name, lo=0, hi=None, st=1):
        if name in PART:
            name, first, w = PART[name]
            lo, hi = first + lo, first + (w if hi is None else hi)
        if hi is None:
            hi = SCRATCH[name][1][1]
        ap = T[name][:, lo:hi] if st == 1 else T[name][:, lo:hi:st]
        if name.startswith("ps"):
            return (ap, [(name, frozenset([0]))])
        return (ap, [(name, frozenset(range(lo, hi, st)))])

    def c1(name, j):
        return a(name, j, j + 1)

    def ind(win, off):
        return (win[0].indirect(off[0]), win[1] + off[1])

    def order(e, reads, writes):
        need = {}
        for kind, accs in (("r", reads), ("w", writes)):
            for x in accs:
                for name, cols_ in x[1]:
                    for k, c, who, sem, val, snap in log.get(name, []):
                        both = k == "r" and kind == "r" and (who == e or not name.startswith("ps"))
                        chain = name.startswith("ps") and who == e and k == kind
                        if both or chain or c.isdisjoint(cols_):
                            continue
                        if val > need.get(sem, (0, None))[0]:
                            need[sem] = (val, snap)
        for sem in sorted(need, key=lambda s: -len(need[s][1])):
            val, snap = need[sem]
            if clock[e].get(sem, 0) < val:
                Q[e].wait_ge(T.sem[sem], val)
                for s, v in snap.items():
                    clock[e][s] = max(clock[e].get(s, 0), v)

    def note(e, reads, writes, sem, inc):
        count[sem] = count.get(sem, 0) + inc
        snap = dict(clock[e]) if e in clock else {}
        snap[sem] = count[sem]
        for kind, accs in (("r", reads), ("w", writes)):
            for x in accs:
                for name, cols_ in x[1]:
                    old = log.get(name, [])
                    if kind == "w":
                        old = [o for o in old if not o[1] <= cols_]
                    log[name] = old + [(kind, cols_, e, sem, count[sem], snap)]

    def op(e, reads, writes, call):
        reads = [x for x in reads if isinstance(x, tuple)]
        order(e, reads, writes)
        call().then_inc(T.sem[SEM[e]], 1)
        note(e, reads, writes, SEM[e], 1)

    def p(x):
        return x[0] if isinstance(x, tuple) else x

    def ts(out, in0, s1, op0, s2=None, op1=None):
        if op1 is None:
            op("v", [in0, s1], [out], lambda: g.vector.tensor_scalar(out[0], in0[0], p(s1), None, op0))
        else:
            op("v", [in0, s1, s2], [out], lambda: g.vector.tensor_scalar(out[0], in0[0], p(s1), p(s2), op0, op1))

    def tt(out, in0, in1, o):
        op("v", [in0, in1], [out], lambda: g.vector.tensor_tensor(out[0], in0[0], in1[0], o))

    def cp(out, in_):
        op("v", [in_], [out], lambda: g.vector.tensor_copy(out[0], in_[0]))

    def scatter(win, off, in_):
        op("v", [in_, off], [win], lambda: g.vector.tensor_copy(win[0].indirect(off[0]), in_[0]))

    def scan(out, d0, d1, init, op0, op1):
        op("v", [d0, d1, init], [out], lambda: g.vector.tensor_tensor_scan(out[0], d0[0], d1[0], p(init), op0, op1))

    def reduce(out, in_, o):
        op("v", [in_], [out], lambda: g.vector.tensor_reduce(out[0], in_[0], AxisListType.X, o))

    def fill(out, v):
        op("v", [], [out], lambda: g.vector.memset(out[0], v))

    def quant(name, lo, hi, in_):
        q, s = a("q" + name, lo, hi), a("s" + name, lo, hi)
        op("v", [in_], [q, s], lambda: g.vector.quantize_mx(q[0], s[0], in_[0]))

    def mm(bank, st, slo, mv, lo, hi, start=True, stop=True):
        o = a("ps%d" % bank, 0, hi - lo)
        x = [a("q" + st, slo, slo + 128), a("s" + st, slo, slo + 128), a("q" + mv, lo, hi), a("s" + mv, lo, hi)]
        op("t", x, [o], lambda: g.tensor.matmul_mx(o[0], x[0][0], x[1][0], x[2][0], x[3][0], start, stop))

    def act(out, in_, f, bias=None, scale=1.0, acc=None):
        kw = {"scale": p(scale)}
        if bias is not None:
            kw["bias"] = p(bias)
        if acc is not None:
            kw["accum_out"] = acc[0]
        op("s", [in_, bias, scale], [out] + ([acc] if acc else []), lambda: g.scalar.activation(out[0], in_[0], f, **kw))

    def lin(out, in_, scale, bias):
        act(out, in_, ACT.Identity, bias, scale)

    def scp(out, in_, scale=1.0):
        act(out, in_, ACT.Copy, None, scale)

    def iota(out, pattern, base=0, cm=0):
        if SCRATCH[out[1][0][0]][2] == I32:
            op("g", [], [out], lambda: g.iota(out[0], pattern, base, cm))
        else:
            op("g", [], [out], lambda: g.iota(out[0], pattern, base, cm, allow_small_or_imprecise_dtypes=True))

    def select(out, in_, pattern, o, base, cm):
        op("g", [in_], [out], lambda: g.affine_select(out[0], in_[0], pattern, o, 0.0, base, cm))

    def dma(e, out, in_, reads, writes, sem):
        order(e, reads, writes)
        Q[e].dma_start(out, in_).then_inc(T.sem[sem], 16)
        note(e, reads, writes, sem, 16)

    def ps(b, lo=0, hi=C):
        return a("ps%d" % b, lo, hi)

    def send(t, what, src):
        way = _route(core, T.cores[(rank + STEP[t]) % n], topo)
        relay = len(way) == 3
        order("g", [src], [])
        if what == "l":
            e = _hop(g, T, topo, core, way[1], T[("rl%d" if relay else "ll%d") % t][:], src[0], "al%d" % t)
        else:
            out = T[what + ("R%d" if relay else "L%d") % t][:]
            if what == "q":
                e = _hop(g, T, topo, core, way[1], out.bitcast(dt.uint8), src[0].bitcast(dt.uint8), "aq%d" % t)
            else:
                e = _hop(g, T, topo, core, way[1], out, src[0], "aq%d" % t)
        count["sent"] = count.get("sent", 0) + e

    for t in range(R):
        e = _engines(topo.mask(_route(T.cores[(rank - STEP[t]) % n], core, topo)[-2], core))
        note("far", [], [a("qL%d" % t), a("sL%d" % t)], "aq%d" % t, 2 * e)
        note("far", [], [a("ll%d" % t)], "al%d" % t, e)

    dma("s", T.ub[:], T.u[:], [], [a("ub")], "du")
    dma("y", a("tw0", 0, 4 * H)[0], T.x[:, 0:4 * H], [], [a("tw0", 0, 4 * H)], "dx")
    dma("y", a("tw0", 4 * H, 4 * C)[0], T.x[:, 4 * H:4 * C], [], [a("tw0", 4 * H, 4 * C)], "dx2")
    dma("y", T.qw[:].bitcast(dt.uint8), T.wc[:], [a("tw0", 4 * H, 4 * H + 8)], [], "dw")
    dma("y", T.sw[:], T.ws[:], [], [a("qw"), a("sw")], "dw")
    dma("y", T.vb[:], T.v[:], [], [a("vb")], "dv")

    c0, c2, c3 = c1("cf", 0), c1("cf", 2), c1("cf", 3)
    b0, bg, b3 = c1("cb", 0), c1("cb", 1), c1("cb", 3)
    K16, c4a, col4, colB, powc, thr0, cz0, c40, c40k, cLV, cy, off16, q103, odd4 = (c1("col", j) for j in range(14))
    f8 = c1("p8", 15)
    iota(a("ip", 0, 1), [[0, 1]], 0, 1)
    iota(a("ip", 8, 16), [[16, 8]], 8, 0)
    iota(a("j16"), [[0, 20], [1, 16]])
    iota(a("I", 0, 68), [[1, 68]])
    iota(a("g8"), [[1, 8], [0, 64]])
    iota(a("q5", 0, 3), [[16 * 103, 3]])
    iota(a("io2"), [[2, C + 32]], -320)
    iota(a("c64"), [[10, 4], [40, 16]], -310)
    iota(a("I", 68, C), [[1, C - 68]], 68)
    iota(a("J"), [[-320, 640]], KEY0)
    iota(a("hk", 128, 256), [[1, 128]], KEY0 - 320 * (320 + 127))
    fill(a("pw", 0, 6), 2.0)
    fill(a("bits"), 0.0)
    ts(c1("ip", 4), c1("ip", 0), 15, ALU.bitwise_and)
    ts(c1("ip", 5), c1("ip", 0), 4, ALU.logical_shift_right)
    ts(c1("ip", 6), c1("ip", 0), 3, ALU.bitwise_and)
    ts(c1("ip", 7), c1("ip", 0), 12, ALU.bitwise_and)
    ts(c1("q5", 20), c1("ip", 0), 1, ALU.bitwise_and)
    scan(a("pw", 8, 14), a("pw", 0, 6), a("pw", 0, 6), 320.0, ALU.mult, ALU.max)
    cp(a("pk"), a("ip", 8, 16))
    cp(a("cb"), a("ip", 4, 8))
    cp(a("cf"), a("ip", 4, 8))
    quant("U", 128, 256, a("bits", 0, 512))
    ts(odd4, c1("q5", 20), 4.0, ALU.mult)
    ts(a("mask"), a("j16"), b0, ALU.is_equal)
    ts(a("nmask"), a("j16"), b0, ALU.not_equal)
    ts(a("h68", 0, 64), a("j16", 0, 64), b0, ALU.is_ge, -1024.0, ALU.mult)
    tt(a("pw", 16, 22), a("pw", 8, 14), a("mask", 0, 6), ALU.mult)
    for x, width, value in ((a("d4"), 80, 0.0), (a("h68", 64, 68), 4, 0.0), (a("W", C, C + 8), 8, 0.0), (a("Ms"), 72, 0.0),
                            (a("z", 64, 68), 4, 0.0), (a("Y"), 96, 0.0), (a("tX", 0, 16), 16, 0.0), (a("es", 0, 5), 5, 0.0),
                            (a("tU", 0, 256), 256, 0.0), (a("neg"), 16, -1.0), (a("d4", 1, 80, 4), 20, -4096.0),
                            (a("d4", 2, 80, 4), 20, -1.0)):
        lin(x, a("bits", 1, 4 * width, 4), 1.0, value)
    for col, scale, bias in ((q103, 103.0, 0.0), (off16, -1024.0, 16384.0), (thr0, 4 * 204800.0, 102400.0), (K16, -K, 15 * K),
                             (cz0, 40.0, -310.0)):
        lin(col, c0, scale, bias)
    quant("u", 0, 128, a("ub"))
    reduce(powc, a("pw", 16, 22), ALU.add)
    pick = a("pk")
    op("s", [a("su"), pick], [a("sS")], lambda: g.scalar.activation(T.sS[:], T.su[:].indirect(pick[0]), ACT.Copy))
    op("v", [a("qu"), pick], [a("qS")], lambda: g.vector.tensor_copy(T.qS[:].bitcast(dt.uint32), T.qu[:].bitcast(dt.uint32).indirect(pick[0])))
    quant("T0", 0, H, a("tw0", 0, 4 * H))
    ts(a("kc", 512, 1024), a("g8"), bg, ALU.is_equal, 320.0, ALU.mult)
    for col, scale, bias in ((c40, 40.0, -319.0), (cy, 40.0, 0.0), (c40k, -40.0, 638.0), (cLV, 8.0, -190.0),
                             (colB, -K / 2, 7.5 * K + 159.5)):
        lin(col, c0, scale, bias)
    lin(c4a, c3, K, c2)
    lin(a("cz", 0, 4), a("I", 0, 4), 204800.0, thr0)
    lin(a("cz", 4, 8), a("I", 0, 4), 10.0, cz0)
    lin(a("cst", 0, 48, 2), a("I", 0, 24), 2.0, c40)
    lin(a("cst", 1, 48, 2), a("I", 0, 24), 2.0, cy)
    lin(a("cdm"), a("I", 0, 20), -2.0, c40k)
    lin(a("ext", 256 + 15, C, 16), a("I", 0, 4), 0.0, K16)
    lin(a("LV"), a("I", 0, 68), 2.0, cLV)
    lin(col4, c4a, 1.0, -12 * K)
    lin(a("kc", 0, 512), a("kc", 512, 1024), 1.0 / 320, 0.0)
    scp(a("M8"), a("nmask"), 8.0)
    lin(a("M16"), a("nmask"), K + BIG, -BIG)
    select(a("kc", 1024, 1536), a("kc", 0, 512), [[1, 128], [0, 4]], ALU.is_gt, 0, -1)
    select(a("kc", 1536, 2048), a("kc", 0, 512), [[-1, 128], [0, 4]], ALU.is_ge, 0, 1)

    def later_constants(step):
        if step == 0:
            quant("k", W320, W320 + 128, a("kc", 512, 1024))
            ts(a("q5", 8, 11), a("q5", 0, 3), q103, ALU.add)
            ts(a("h68", 16, 68, 16), a("h68", 16, 68, 16), off16, ALU.add)
            iota(a("I", C, C + H), [[1, H]])
            iota(a("TL", 0, L), [[1, L]], 320)
            iota(a("TL", L, C), [[0, C - L]])
            iota(a("pr"), [[1, 16], [16, 20]])
            for b in range(4):
                select(a("E", 512 * b, 512 * b + 512), a("kc", 0, 512), [[-1, 512]], ALU.is_equal, b, 4)
        if step == 1:
            ts(a("q5", 16, 19), a("q5", 8, 11), 10, ALU.logical_shift_right)
            scan(a("p8"), a("M8", 0, 16), a("neg"), 0.0, ALU.mult, ALU.min)
        if step == 2:
            ts(a("xl", 4, 7), a("q5", 16, 19), 3.0, ALU.min, 64.0, ALU.add)
            ts(a("xl", 0, 3), a("q5", 16, 19), 3.0, ALU.min, odd4, ALU.max)
        if step == 3:
            quant("k", PRE, PRE + 256, a("kc", 1024, 2048))
            quant("k", ONE, ONE + 128, a("kc", 0, 512))
        if step >= 4:
            for j in (2 * step - 8, 2 * step - 7):
                ts(a("nm4", 80 * j, 80 * j + 80), a("j16", 0, C, 4), b3, ALU.not_equal)
        if step == 5:
            lin(a("M4"), a("nm4"), K + BIG, -BIG)

    ACC = {"A": 0, "B": 24}
    BANK = {"A": 3, "B": 6}
    STAT = {"A": W320, "B": ONE}

    def rows(x, k):
        w = 64 * (k + 1)
        for j in range(4):
            if k == 0:
                o = a("t0", j, 256, 4)
            elif k == 1:
                o = a("tU", 256 + j, 256 + 4 * w, 4)
            else:
                o = a("t" + x, TILE[k][0] + j, TILE[k][0] + 4 * w, 4)
            m = 4 * k + j
            if x == "A":
                act(o, ps(5 if w <= H else 0, 0, w), ACT.Sign, c1("sx", 16 * m + 15), -1.0, c1("acc", m))
            else:
                act(o, a("kB", 0, w), ACT.Sign, c1("kx", 16 * m + 15), f8, c1("acc", ACC[x] + m))

    def pack(x, k):
        if x == "A" and k < 2:
            quant("A", 576 + 128 * k, 704 + 128 * k, a("tA", 3072 + 512 * k, 3584 + 512 * k))
        elif k == 1:
            quant("U", 0, 128, a("tU", 0, 512))
        else:
            quant(x, TILE[k][1], TILE[k][1] + 64 * k, a("t" + x, TILE[k][0], TILE[k][0] + 256 * k))

    def cols(x, k, start=False, stop=False):
        if x == "A" and k < 2:
            mm(BANK[x], "k", STAT[x], x, 576 + 128 * k, 704 + 128 * k, start, stop)
            return
        if k == 1:
            mm(BANK[x], "k", STAT[x], "U", 64, 192, start, stop)
            return
        if k == 4:
            mm(4, "k", STAT[x], x, 128, 256, start, True)
        mm(BANK[x], "k", STAT[x], x, TILE[k][1], TILE[k][1] + min(64 * k, 192), start, stop)

    def wrap(out, row, lo, hi):
        scan(a(out, lo, hi), a("M16", 0, hi - lo), row, 0.0, ALU.add, ALU.max)

    def keysA(bank, lo, hi, step):
        if step == 0:
            tt(a("sm", lo, hi), ps(bank, 0, hi - lo), a("mask", 0, hi - lo), ALU.mult)
        else:
            scan(a("sx", lo, hi), a("nmask", 0, hi - lo), a("sm", lo, hi), 0.0, ALU.mult, ALU.add)

    def keysB(lo, hi, step):
        at = (lo + 128) % C
        u, part, row = a("ul", lo // 16, hi // 16), a("hk", at, at + hi - lo), a("kB", at, at + hi - lo)
        if step == 0:
            ts(u, a("acc", lo // 16, hi // 16), 320.0, ALU.add)
        elif step == 1:
            tt(part, ind(a("J"), u), a("I", lo, hi), ALU.add)
        elif step == 2:
            tt(row, ps(4, lo - 128, hi - 128) if lo else ps(3, lo, hi), part, ALU.add)
        else:
            scan(a("kx", at, at + hi - lo), a("M8", 0, hi - lo), row, 0.0, ALU.mult, ALU.max)

    def positions(lo, hi, step):
        d, u = a("sm2", lo // 16, hi // 16), a("ul", 20 + lo // 16, 20 + hi // 16)
        if step == 0:
            tt(d, a("acc", 24 + lo // 16, 24 + hi // 16), a("ext", lo + 15, hi, 16), ALU.subtract)
        elif step == 1:
            ts(u, d, 0.5, ALU.mult, colB, ALU.add)
        else:
            scatter(a("orow"), u, a("I", 192 + lo, 192 + hi))

    def w(lo, hi=None):
        return a("W", C + lo, C + (lo + 1 if hi is None else hi))

    def share(m0, m1):
        for m in range(m0, m1):
            ts(a("tA", 3072 + 512 * (m // 4) + m % 4, 3584 + 512 * (m // 4), 4), ps(6, 0, 128), c1("sx", 16 * m + 15), ALU.is_lt, 2.0, ALU.mult)

    def levels(m0, m1):
        for m in range(m0, m1):
            ts(a("tX", 4 * (5 - m % 5) + m // 5, 4 * C + 4, 20), a("LV", m // 5, m // 5 + 64), c1("sm2", 60 + m), ALU.add, c1("h2", m), ALU.is_equal)

    def same(out, k):
        tt(out, a("dm", 5 * k, 20), a("dm", 0, 20 - 5 * k), ALU.is_equal)

    def bits(bank, lo, hi):
        ts(a("bits", 4 * lo, 4 * hi, 4), ps(bank, 0, hi - lo), 0.0, ALU.is_gt, powc, ALU.mult)

    def add(bank, lo, hi, b):
        tt(a("tmp", 4 * lo + b, 4 * hi, 4), ps(bank + b, 0, hi - lo), a("V64", 4 * lo + b, 4 * hi, 4), ALU.add)

    def unpack(t):
        for b, bank in enumerate((2, 3, 5, 7)):
            mm(bank, "E", 128 * b, "L%d" % t, 0, C)
        for b, bank in enumerate((2, 3, 5, 7)):
            scp(a("D", b, 4 * C, 4), ps(bank))

    def new_state(t):
        tw, nx, ll = "tw%d" % t, "tw%d" % (t + 1), "ll%d" % t

        def down(lo, hi, b):
            if b < 3:
                scp(a(nx, 4 * lo + b, 4 * hi, 4), a("tmp", 4 * lo + b, 4 * hi, 4), 0.015625)
            else:
                ts(a(nx, 4 * lo + b, 4 * hi, 4), a("tmp", 4 * lo + b, 4 * hi, 4), 0.015625, ALU.mult)

        cp(a(tw, 4 * C, 4 * C + 2 * L), ind(a("D"), a(ll, 0, 12)))
        scp(a(tw, 4 * C + 2 * L, 4 * C + 4 * L), ind(a("D"), a(ll, 12, 24)))
        scp(a("V", 448, 4 * H), ind(a(tw), a("off", 28, 48)))
        cp(a("V", 0, 448), ind(a(tw), a("off", 0, 28)))
        scp(a("V", 4 * H, 4 * C), ind(a(tw), a("off", 48, 80)))
        quant("V", 0, H, a("V", 0, 4 * H))
        ts(a("V64", 0, 4 * H), a("V", 0, 4 * H), 64.0, ALU.mult)
        for b in range(4):
            mm(4 + b, "w", 128 * b, "V", 0, H)
        quant("V", H, C, a("V", 4 * H, 4 * C))
        scp(a("V64", 4 * H, 4 * C), a("V", 4 * H, 4 * C), 64.0)
        for b in range(4):
            mm(b, "w", 128 * b, "V", H, C)
        for b in range(4):
            add(4, 0, H, b)
            if b < 3:
                down(0, H, b)
        add(0, H, C, 0)
        add(0, H, C, 1)
        down(0, H, 3)
        add(0, H, C, 2)
        add(0, H, C, 3)
        for b in range(3):
            down(H, C, b)
        quant("T%d" % (t + 1), 0, H, a(nx, 0, 4 * H))
        down(H, C, 3)

    uC, uP, uD, uL, uS = (a("ul", lo, hi) for lo, hi in ((40, 60), (60, 80), (80, 100), (100, 106), (106, 110)))
    zeros = a("bits", 1, 4 * C, 4)
    cnt, red, pos2, free = w(0, 4), c1("es", 36), a("Yo", 2, 80, 4), a("sm2", 60, 80)

    for t in range(R):
        tw, qT = "tw%d" % t, "T%d" % t
        first = t == 0

        mm(6, "S", 0, qT, 0, H)
        mm(7, "u", 0, qT, 0, H)
        mm(5, "S", 0, qT, 0, H)
        quant(qT, H, C, a(tw, 4 * H, 4 * C))
        mm(1, "u", 0, qT, H, C)
        mm(4, "S", 0, qT, H, C)
        send(t, "q", a("q" + qT))
        send(t, "s", a("s" + qT))
        if first:
            later_constants(0)
        keysA(6, 0, H, 0)
        bits(7, 0, H)
        keysA(6, 0, H, 1)
        bits(1, H, C)
        quant("bits", 0, H, a("bits", 0, 4 * H))
        rows("A", 2)
        quant("bits", H, C, a("bits", 4 * H, 4 * C))
        mm(3, "k", W320, "bits", 0, 192, True, False)
        mm(2, "k", W320, "bits", 0, C)
        mm(7, "k", W320, "bits", 0, C)
        mm(0, "S", 0, qT, 0, C)
        share(4, 8)
        keysA(4, H, C, 0)
        if first:
            later_constants(1)

        for j in range(1, 4):
            act(a("tB", j, 4 * C, 4), ps(2), ACT.Sign, c1("cz", j), -1.0, w(j))
        ts(a("tB", 0, 4 * C, 4), ps(7), c1("cz", 0), ALU.is_le, 2.0, ALU.mult)
        keysA(4, H, C, 1)
        mm(4, "k", W320, "bits", 128, C, True, False)
        if first:
            later_constants(2)
        scan(a("W", 1, C + 1), a("tB", 0, 4 * C, 4), zeros, -320.0, ALU.add, ALU.add)
        rows("A", 4)
        pack("A", 1)
        keysB(128, H, 0)

        ts(uS, cnt, 0.5, ALU.mult, 160.0, ALU.add)
        share(2, 4)
        tt(a("z", 65, 68), w(0, 3), a("cz", 4, 7), ALU.subtract)
        tt(a("z", 0, 64), ind(a("io2"), uS), a("c64"), ALU.subtract)
        share(0, 2)
        tt(a("pre"), ind(w(0, 8), a("xl", 0, 3)), a("cst"), ALU.subtract)
        rows("A", 3)
        lin(a("Sg"), ind(a("io2"), uS), 1.0, 319.0)
        scan(a("Ms", 0, 68), a("h68"), a("z"), 0.0, ALU.add, ALU.min)
        reduce(red, a("z", 0, 64), ALU.min)
        pack("A", 2)
        pack("A", 0)
        tt(a("Y", 0, 96, 2), ind(a("Ms"), a("xl", 4, 7)), a("pre"), ALU.subtract)
        ts(a("Y", 1, 80, 4), a("pre", 0, 40, 2), red, ALU.subtract, -639.0, ALU.add)
        keysB(128, H, 1)
        scan(a("Yo"), a("d4"), a("Y", 0, 80), 0.0, ALU.mult, ALU.max)
        pack("A", 4)
        for k in (0, 1, 2, 4):
            cols("A", k)

        for m in range(20):
            act(a("hs", 64 * m, 64 * m + 64), a("Sg"), ACT.Sign, c1("Yo", 4 * m + 2), -1.0, c1("h2", m))
        ts(free, a("Yo", 0, 80, 4), 0.0, ALU.is_gt, 128.0, ALU.mult)
        keysB(H, C, 0)
        pack("A", 3)
        cols("A", 3, stop=True)
        keysB(H, C, 1)
        levels(0, 5)
        keysB(H, C, 2)
        keysB(0, H, 2)
        levels(5, 10)
        keysB(0, H, 3)
        rows("B", 4)
        levels(10, 20)
        tt(a("sm2", 20, 40), a("h2"), free, ALU.subtract)
        ts(uP, pos2, 0.5, ALU.mult)
        if first:
            later_constants(3)

        quant("X", 0, C, a("tX", 4, 4 * C + 4))
        mm(1, "k", PRE, "X", 0, C, True, False)
        ts(a("sm2", 80, 100), a("sm2", 20, 40), 5.0, ALU.mult)
        quant("X", C, 2 * C, a("tX", 0, 4 * C))
        mm(1, "k", SUF, "X", C, 2 * C, False, True)
        rows("B", 3)
        tt(a("dm"), a("sm2", 80, 100), a("cdm"), ALU.add)
        keysB(H, C, 3)
        pack("B", 4)
        cols("B", 4, start=True)
        same(a("es", 20, 30), 2)
        ts(uD, a("dm"), 0.5, ALU.mult, 160.0, ALU.add)
        same(a("es", 5, 20), 1)
        scan(a("G"), ps(1), zeros, 0.0, ALU.add, ALU.add)
        tt(a("es", 10, 20), a("es", 10, 20), a("es", 20, 30), ALU.add)
        rows("B", 1)
        rows("B", 2)
        same(a("es", 30, 35), 3)
        wrap("ext", ps(4, 64, 128), 192, 256)
        cp(a("Gg"), ind(a("G"), uD))
        tt(a("es", 15, 20), a("es", 15, 20), a("es", 30, 35), ALU.add)
        positions(192, C, 0)
        pack("B", 3)
        wrap("ext", a("Gg"), C, 2 * C)
        positions(192, C, 1)
        pack("B", 1)
        scp(a("prow"), ind(a("I", 0, C), uP))
        rows("B", 0)
        tt(a("sm2", 40, 60), a("ext", C + 15, 2 * C, 16), a("es", 0, 20), ALU.add)
        pack("B", 2)
        cols("B", 1)
        cols("B", 3)
        cols("B", 2, stop=True)
        positions(192, C, 2)
        ts(uC, a("sm2", 40, 60), K16, ALU.subtract)
        wrap("ext", ps(6, 0, 192), 0, 192)

        scp(a("TLg"), ind(a("TL"), uC))
        scatter(a("lp"), uC, a("prow"))
        positions(0, 192, 0)
        if not first:
            scp(a("TLn"), ind(a("TLg"), a("pm")))
            unpack(t)
        if first:
            later_constants(4)
        wrap("eo", a("lp", 0, L), C + L, C + 2 * L)
        positions(0, 192, 1)
        if first:
            later_constants(5)
        ts(uL, a("eo", C + L + 15, C + 2 * L, 16), K16, ALU.subtract)
        positions(0, 192, 2)
        if first:
            wrap("px", a("pr"), 0, C)
        scp(a("otj"), ind(a("orow"), uP))
        cp(a("brow"), ind(a("orow"), uL))
        if first:
            ts(a("pm"), a("px", 15, C, 16), K16, ALU.subtract)
            scp(a("TLn"), ind(a("TLg"), a("pm")))
        scan(a("eo", C, C + L), a("M4", 0, L), a("brow"), 0.0, ALU.add, ALU.max)
        ts(a("sl%d" % t), a("eo", C + 3, C + L, 4), 4.0, ALU.mult, col4, ALU.add)
        send(t, "l", a("sl%d" % t))

        if first:
            quant("E", 0, 512, a("E"))
            unpack(t)
        tt(a("otr"), ind(a("otj"), a("pm")), a("TLn"), ALU.max)
        if first:
            quant("v", 0, 128, a("vb"))
        scan(a("eo", 0, C), a("M4"), a("otr"), 0.0, ALU.add, ALU.max)
        ts(a("off"), a("eo", 3, C, 4), 4.0, ALU.mult, col4, ALU.add)
        if t == R - 1:
            dma("y", T.ot[:], T.otr[0:128:16, :], [a("otr")], [], "dout")
        new_state(t)

    last = "T%d" % R
    mm(4, "v", 0, last, 0, H)
    dma("y", T.oc[:, 0:4 * H], T["q" + last][:, 0:H].bitcast(dt.uint8), [a("q" + last, 0, H)], [], "dout")
    quant(last, H, C, a("tw%d" % R, 4 * H, 4 * C))
    mm(5, "v", 0, last, H, C)
    scp(a("yb", 0, H), ps(4, 0, H))
    cp(a("yb", H, C), ps(5, 0, C - H))
    dma("s", T.y[:, 0:H], a("yb", 0, H)[0], [a("yb", 0, H)], [], "dout")
    dma("y", T.oc[:, 4 * H:4 * C], T["q" + last][:, H:C].bitcast(dt.uint8), [a("q" + last, H, C)], [], "dout")
    for k in range(4):
        dma("ys"[k % 2], T.osc[4 * k:4 * k + 4, :], T["s" + last][32 * k:32 * k + 4, :], [a("s" + last)], [], "dout")
    dma("y", T.y[:, H:C], a("yb", H, C)[0], [a("yb", H, C)], [], "dout")
    for sem in count:
        g.wait_ge(T.sem[sem], count[sem])
